import numpy as np, ml_dtypes
CORES = [24,25,26,27,28,29,30,31]
N = 8
BF = ml_dtypes.bfloat16
def gentries(a):
    return np.ascontiguousarray(a.reshape(8, 16, -1).transpose(0, 2, 1)).reshape(8, -1)
def gtable(e):
    e = np.asarray(e); return np.ascontiguousarray(e.reshape(8, -1, 16).transpose(0, 2, 1)).reshape(128, -1).astype(np.int32)
V, G, CAP, D, SH, RO = 2048, 256, 64, 2, 2, 4
def parts(rng):
    t = rng.integers(2 ** 18, 2 ** 19, (N, 8, 16, 1))
    r = np.minimum((t * rng.random((N, 8, 1, V)) * rng.random((N, 8, 16, V))).astype(np.int64), t - 1)
    nb = rng.integers(0, V + (N - 1) * G, (N, 8, D * V)); snd = np.argsort(rng.random((N, 8, N - 1, V)), axis=-1)[..., :G]
    return t, r, nb, np.ascontiguousarray(snd)
def heat(rng, t, r, share):
    m = (rng.random((N, 8, 1, V)) < share) & (rng.random(r.shape) < rng.random((N, 8, 1, V)))
    return np.where(m, np.minimum(t + ((2 ** 20 - t) * rng.random(r.shape)).astype(np.int64), 2 ** 20 - 1), r)
def pack(t, r, nb, snd):
    return {"r0": np.ascontiguousarray(r.reshape(N, 128, V)).astype(np.int32), "th": np.ascontiguousarray(t.reshape(N, 128, 1)).astype(np.int32),
            "nb": np.stack([gtable(a) for a in nb]), "snd": np.stack([gtable(a.reshape(8, -1)) for a in snd])}
def setup_inputs(rng):
    t, r, nb, snd = parts(rng); share = rng.choice(np.array([0.05, 0.15, 0.3, 0.5]), (N, 8, 1, 1))
    return pack(t, heat(rng, t, r, share), nb, snd)
def setup_inputs_room(rng):
    t, r, nb, snd = parts(rng); h = V // 2
    for q in range(N):
        for g in range(8):
            o = rng.permutation(V); a, b = o[:h], o[h:]; i = rng.integers(0, 16, h); lo = t[q, g, i, 0]
            r[q, g, i, a] = np.where(rng.random(h) < 0.5, lo, np.minimum(lo + ((2 ** 20 - lo) * rng.random(h)).astype(np.int64), 2 ** 20 - 1))
            for d in range(N - 1):
                n = int(rng.choice(np.array([0, 1, CAP - 1, CAP, CAP + 1, G])))
                if q == 0 and d == 0: n = (CAP, CAP + 1, G, CAP - 1, 1, 0, CAP, CAP + 1)[g]
                snd[q, g, d] = rng.permutation(np.concatenate([rng.permutation(a)[:n], rng.permutation(b)[:G - n]]))
    return pack(t, r, nb, snd)
def setup_inputs_ties(rng):
    t, r, nb, snd = parts(rng)
    base = rng.choice(np.array([1, 4, 7, 1000, 2 ** 16 - 1, 2 ** 19, 2 ** 20 - 1]), (N, 8, 1, 1)); base[0, 0] = 1; base[0, 1] = 2 ** 19; base[1, 0] = 2 ** 20 - 1
    t = np.minimum(base + rng.integers(0, 3, (N, 8, 16, 1)), 2 ** 20)
    r = (t - 1) * rng.integers(0, 2, (N, 8, 16, V)); hit = rng.random((N, 8, 1, V)) < 0.2
    r = np.where(hit, np.minimum(t - 1 + rng.integers(0, 3, r.shape), 2 ** 20 - 1), r)
    m = rng.permutation(V)[None, :]
    r[0, 0] = np.where(m < 3 * V // 10, t[0, 0], np.where(m < 6 * V // 10, rng.integers(2 ** 19, 2 ** 20, (16, V)), t[0, 0] - 1))
    return pack(t, r, nb, snd)
def setup_inputs_alike(rng):
    t, r, nb, snd = parts(rng); r = heat(rng, t, r, 0.2); r[..., 0] = 2 ** 20 - 1; r[..., V - 1] = 2 ** 20 - 1
    snd[:, ::2] = rng.choice(np.array([0, V - 1, V // 2, 3]), (N, 4, N - 1, G))
    nb[:, 1::2] = np.tile(nb[:, 1::2, :V], (1, 1, D))
    nb[:, 2] = rng.integers(V, V + (N - 1) * G, (N, D * V)); nb[:, 4] = rng.integers(0, V, (N, D * V))
    nb[:, 6] = rng.choice(np.array([0, V - 1, V, V + (N - 1) * G - 1]), (N, D * V))
    return pack(t, r, nb, snd)
def setup_inputs_cold(rng):
    t, r, nb, snd = parts(rng); share = rng.choice(np.array([0.1, 0.25, 0.4]), (N, 8, 1, 1))
    q = rng.permutation(N); share[q[0]] = 1.0; share[q[1]] = 0.0; share[:, rng.integers(0, 8)] = 0.0
    return pack(t, heat(rng, t, r, share), nb, snd)
def setup_inputs_spread(rng):
    t, r, nb, snd = parts(rng)
    t = np.minimum(np.maximum(np.exp2(10 + 10 * rng.random((N, 8, 16, 1))).astype(np.int64), 1), 2 ** 20)
    r = np.minimum((np.exp2(20 * rng.random((N, 8, 1, V))) * rng.random((N, 8, 16, V))).astype(np.int64), 2 ** 20 - 1)
    return pack(t, r, nb, snd)
def check_inputs(d):
    bad = []
    for k, lo, hi in (("r0", 0, 2 ** 20 - 1), ("th", 1, 2 ** 20), ("nb", 0, V + (N - 1) * G - 1), ("snd", 0, V - 1)):
        if np.min(d[k]) < lo or np.max(d[k]) > hi: bad.append("range of " + k)
    return bad
def reference(r0, th, nb, snd):
    r = r0.astype(np.int64).reshape(N, 8, 16, V); t = th.astype(np.int64).reshape(N, 8, 16, 1); p = np.zeros((N, 8, 16, V), np.int64)
    nbl = np.stack([gentries(a) for a in nb]).astype(np.int64); sl = np.stack([gentries(a) for a in snd]).astype(np.int64).reshape(N, 8, N - 1, G)
    for rnd in range(RO):
        over = r >= t; s = np.where(over, r >> SH, 0)
        p = p + np.where(over, r - D * s, 0); r = np.where(over, 0, r)
        hot = np.any(over, axis=2)
        come = []
        for a in range(N):
            w = [s[a]]
            for d in range(1, N):
                q = (a - d) % N; ix = sl[q, :, d - 1]
                h = np.take_along_axis(hot[q], ix, 1).astype(np.int64); before = np.add.accumulate(h, axis=1) - h
                v = np.take_along_axis(s[q], ix[:, None, :], 2)
                w.append(np.where(((h == 1) & (before < CAP))[:, None, :], v, 0))
            w = np.concatenate(w, axis=2)
            come.append(np.add.reduce(np.take_along_axis(w, nbl[a][:, None, :], 2).reshape(8, 16, D, V), axis=2))
        r = r + np.stack(come)
    return {"yp": p.reshape(N, 128, V).astype(np.float32), "yr": r.reshape(N, 128, V).astype(np.float32)}

@@ -1,0 +1,403 @@
+import numpy as np
+from concourse.bass import DstId, RemoteDMATransfer
+from concourse.mybir import AluOpType, ActivationFunctionType
+
+V, G, N, RO, CAP = 2048, 256, 8, 4, 64
+NS = (N - 1) * G
+NC = NS // 16
+PAD = 8
+BIG = 4096.0
+SCRATCH = {
+    "r0i": ("sbuf", [128, V], "int32"),
+    "thi": ("sbuf", [128, 1], "int32"),
+    "thb": ("sbuf", [128, 1], "float32"),
+    "thc": ("sbuf", [128, 1], "float32"),
+    "nbi": ("sbuf", [128, 256], "int32"),
+    "nbu": ("sbuf", [128, 256], "uint16"),
+    "sni": ("sbuf", [128, NC], "int32"),
+    "snf": ("sbuf", [128, NC], "float32"),
+    "snu": ("sbuf", [128, NC], "uint16"),
+    "qf": ("sbuf", [128, NC], "float32"),
+    "lstu": ("sbuf", [128, NC], "uint16"),
+    "one": ("sbuf", [128, 144], "bfloat16"),
+    "bk1": ("sbuf", [128, 144], "bfloat16"),
+    "bk2": ("sbuf", [128, 144], "bfloat16"),
+    "sel": ("sbuf", [128, 144], "bfloat16"),
+    "tri1": ("sbuf", [128, 128], "bfloat16"),
+    "tri": ("sbuf", [128, 128], "bfloat16"),
+    "blkn": ("sbuf", [128, 128], "bfloat16"),
+    "rm": ("sbuf", [128, NC], "bfloat16"),
+    "hb": ("sbuf", [128, NC], "bfloat16"),
+    "cs": ("sbuf", [128, NC], "bfloat16"),
+    "RA": ("sbuf", [128, V], "float32"),
+    "RB": ("sbuf", [128, V], "float32"),
+    "X": ("sbuf", [128, V], "float32"),
+    "TT": ("sbuf", [128, V], "float32"),
+    "U0": ("sbuf", [128, V], "float32"),
+    "U1": ("sbuf", [128, V], "float32"),
+    "E0": ("sbuf", [128, V], "float32"),
+    "E1": ("sbuf", [128, V], "float32"),
+    "gs": ("sbuf", [128, NS], "bfloat16"),
+    "ob0": ("sbuf", [128, NS], "float32"),
+    "ob1": ("sbuf", [128, NS], "float32"),
+    "W0": ("sbuf", [128, PAD + V + NS], "float32"),
+    "W1": ("sbuf", [128, PAD + V + NS], "float32"),
+    "W2": ("sbuf", [128, PAD + V + NS], "float32"),
+    "W3": ("sbuf", [128, PAD + V + NS], "float32"),
+    "AB": ("psum", [128, V], "float32"),
+    "hot": ("psum", [128, V], "float32"),
+}
+SEMAPHORES = (["vq", "sq", "pq", "gq", "lsa", "lsb", "lth", "lsn", "lnb", "outp", "outr"] + ["lr%d" % c for c in range(4)]
+              + ["arr%d" % t for t in range(RO)] + ["acc%d" % k for k in range(2 * RO)])
+
+STAGES = ((0, 1), (1, 2), (3, 2), (5, 2))
+PARTS = ((0, 3), (3, 4))
+
+ORD = {
+    "start": {"v": "c0 c1 lst c2 c3 G0 X0 X1 X2 X3 H0 C0 Q0 L0 M1 M3 nb".split(),
+              "s": "A0 A1 A2 A3 G1 W0 W1 W2 W3 M0 M2".split()},
+    "step": {"v": "ub ua r0 u1 u2 r1 u3 r2 r3 G0 X0 X1 X2 X3 H0 C0 Q0 L0 M1 M3".split(),
+             "s": "tb ta t1 t2 t3 A0 A1 A2 A3 G1 W0 W1 W2 W3 M0 M2".split()},
+    "wait": {"v": "d1 d0 b0".split(), "s": "e1 e0 b1".split()},
+    "wait3": {"v": "d1 d0 v1 v0 f1 f0".split(), "s": "e0 e1 b1 b0".split()},
+    "end": {"v": "ua ub u1 r0 u2 r1 r2 u3 r3 p3".split(),
+            "s": "ta tb t1 t2 p0 p1 t3 q0 q1 p2 q2 q3".split()},
+}
+OUT = "p0 p1 q0 q1 p2 q2 p3 q3".split()
+
+
+def order(q, T, topo):
+    far = [d for d in range(1, N) if topo.die(T.cores[(q + d) % N]) != topo.die(T.cores[q])]
+    near = [d for d in range(1, N) if d not in far]
+    far.sort(key=lambda d: abs(d - N // 2))
+    o = []
+    for k in range(N):
+        if k < len(far):
+            o.append(far[k])
+        if k < len(near):
+            o.append(near[k])
+    return o
+
+
+def lanes(q, T, topo):
+    o, res = order(q, T, topo), {}
+    for first, n in STAGES:
+        for k in range(n):
+            e = topo.engines(T.cores[q], T.cores[(q + o[first + k]) % N])
+            res[o[first + k]] = e[k::n]
+    return res
+
+
+def rank_program(g, core, T, topo):
+    q = T.rank_of(core)
+    if q is None:
+        return
+    v, s, pe, sy = g.vector, g.scalar, g.tensor, g.sync
+    eng = {"g": g, "v": v, "s": s, "p": pe, "y": sy}
+    cnt, seen, tok = {}, {}, {}
+    op, fn = AluOpType, ActivationFunctionType
+    LAM = 2.0 ** -21
+    SC = 2.0 ** 22
+    ONE = 1.0 - 2.0 ** -23
+    Q4 = 0.25 * ONE
+    NST = len(STAGES)
+
+    def need(k, *toks):
+        for name, val in toks:
+            if seen.get((k, name), 0) < val:
+                eng[k].wait_ge(T.sem[name], val)
+                seen[(k, name)] = val
+
+    def fin(ins, name, n=1):
+        cnt[name] = cnt.get(name, 0) + n
+        ins.then_inc(T.sem[name], n)
+        return (name, cnt[name])
+
+    o, lane = order(q, T, topo), lanes(q, T, topo)
+    arrive = sum(len(lanes((q - d) % N, T, topo)[d]) for d in range(1, N))
+    C = [slice(512 * c, 512 * c + 512) for c in range(4)]
+    CW = [slice(PAD + 512 * c, PAD + 512 * c + 512) for c in range(4)]
+    HF = [slice(1024 * h, 1024 * h + 1024) for h in range(2)]
+    HW = [slice(PAD + 1024 * h, PAD + 1024 * h + 1024) for h in range(2)]
+    ALL = slice(PAD, PAD + V + NS)
+    W = [T["W%d" % t] for t in range(RO)]
+    U, E, OB = [T.U0, T.U1], [T.E0, T.E1], [T.ob0, T.ob1]
+    R = [T.RA, T.RB, T.RB, T.RB, T.RB]
+    PIECE = {"a": (0, 256), "b": (256, 256), "1": (512, 512), "2": (1024, 512), "3": (1536, 512)}
+    HC, YC = slice(0, NC), slice(512, 512 + NC)
+    left = {}
+
+    def cols(a, n):
+        return slice(G * a, G * (a + n)), slice(16 * a, 16 * (a + n))
+
+    def send(i, t):
+        a, n = STAGES[i]
+        ls = "ls" + "ab"[t % 2]
+        tr = []
+        for k in range(n):
+            d = o[a + k]
+            dst = T.cores[(q + d) % N]
+            ad = topo.addr(dst)
+            m = sum(1 << e for e in lane[d])
+            src = OB[t % 2][:, G * (a + k):G * (a + k + 1)]
+            out = W[t][:, PAD + V + (d - 1) * G:PAD + V + d * G]
+            cnt[ls] = cnt.get(ls, 0) + len(lane[d])
+            if n == 1:
+                g.remote_dma(out, src, T.sem["arr%d" % t], T.sem[ls], ad[1], ad[0], m)
+            else:
+                tr.append(RemoteDMATransfer(dst_ids=[DstId(rid=ad[0], pnc=ad[1])], dma_engine_mask=m,
+                                            remote_sem=T.sem["arr%d" % t], src=src, dst=out))
+        if tr:
+            g.remote_dma_fused(tr, local_sem=T.sem[ls])
+        left[t] = cnt[ls]
+
+    tok["th"] = fin(s.dma_start(T.thi[:], T.th[:]), "lth", 16)
+    for c in range(4):
+        tok["l%d" % c] = fin(sy.dma_start(T.r0i[:, C[c]], T.r0[:, C[c]]), "lr%d" % c, 16)
+    tok["sn"] = fin(s.dma_start(T.sni[:], T.snd[:]), "lsn", 16)
+    tok["nbl"] = fin(s.dma_start(T.nbi[:], T.nb[:]), "lnb", 16)
+    k1 = fin(v.memset(T.one[:], 1.0), "vq")
+    need("g", k1)
+    k2 = fin(g.affine_select(T.bk1[:], T.one[:], [[-16, 9], [0, 16]], op.is_ge, 0.0, 0, 1), "gq")
+    tok["rm"] = fin(g.affine_select(T.rm[:], T.one[:, 0:NC], [[0, N - 1], [1, 16]], op.is_gt, 0.0, 0, 0), "gq")
+    need("g", k2)
+    k3 = fin(g.affine_select(T.bk2[:], T.bk1[:], [[16, 9], [0, 16]], op.is_ge, 0.0, 15, -1), "gq")
+    need("g", k3)
+    tok["sel"] = fin(g.affine_select(T.sel[:], T.bk2[:], [[0, 9], [1, 16]], op.is_equal, 0.0, -15, 0), "gq")
+    k4 = fin(g.affine_select(T.tri1[:], T.bk2[:, 0:128], [[-1, 128]], op.is_gt, 0.0, 0, 1), "gq")
+    for t in range(RO):
+        tok["pad"] = fin(v.memset(W[t][:, 0:PAD], 4.0), "vq")
+    need("v", tok["th"])
+    tok["thb"] = fin(v.tensor_scalar(T.thb[:], T.thi[:], -2.0, 4.0, op.mult, op.add), "vq")
+    tok["thc"] = fin(v.tensor_scalar(T.thc[:], T.thi[:], -1.0, LAM, op.add, op.mult), "vq")
+
+    def deps(x, t):
+        a, b = x[0], x[1:]
+        al = ["0", "1", "2", "3"]
+        gp = [str(i) for i in range(len(PARTS))]
+        st = [str(i) for i in range(NST)]
+        if a == "c":
+            return ["l" + b]
+        if x == "nb":
+            return ["nbl"]
+        if x == "mat":
+            return ["mat0"]
+        if x == "lst":
+            return ["sn"]
+        if a == "A":
+            return ["thb", "thc", ("r" + b, t - 1)]
+        if a == "X":
+            return [("A" + b, t), ("r" + b, t - 1), ("W" + b, t - 1)]
+        if a == "W":
+            return [("X" + b, t)]
+        if a == "G":
+            return ["thb", "thc", "lst"] + [("r" + c, t - 1) for c in al] + [("P" + b, t - 1)]
+        if a == "P":
+            return ["sel", ("G" + b, t), ("H0", t - 1)]
+        if a == "H":
+            return [("P" + i, t) for i in gp] + [("C0", t - 1), ("K0", t - 1)]
+        if a == "C":
+            return ["rm", ("H0", t), ("K0", t - 1)]
+        if a == "K":
+            return ["mat", ("C0", t), ("Q0", t - 1)]
+        if a == "Q":
+            return [("K0", t), ("L0", t - 1)]
+        if a == "L":
+            return [("Q0", t)] + [("M" + i, t - 1) for i in st]
+        if a == "M":
+            return ["pad", ("L0", t)] + [("W" + c, t) for c in al] + [("left", t - 2)]
+        if a == "S":
+            return [("M" + b, t)]
+        if a == "d":
+            return [("X" + str(2 * int(b) + h), t) for h in range(2)]
+        if a == "b":
+            return [("d" + b, t)]
+        if a == "e":
+            w2 = [("W" + c, t) for c in (al[:2] if b == "0" else al[2:])]
+            if t == RO - 1:
+                return w2 + [("Q0", t)]
+            return w2 + [("Y", t - 2)]
+        if a == "Y":
+            return [("e0", t), ("e1", t), ("d0", t), ("d1", t), ("Z", t - 1)] + [("G" + i, t) for i in gp]
+        if a == "Z":
+            return [("Y", t)] + [("u" + c, t) for c in "ab123"]
+        if a == "t":
+            return ["nb", ("arr", t)] + [("W" + c, t) for c in al] + [("u" + b, t - 1)]
+        if a == "u":
+            return ["nb", ("arr", t)] + [("W" + c, t) for c in al] + [("t" + b, t), ("Z", t - 2)]
+        if a == "r":
+            return [("b" + str(int(b) // 2), t)] + [("u" + c, t) for c in ("ab" if b == "0" else b)]
+        if a == "v":
+            return [("e" + b, t), ("Z", t - 1)] + [("W" + c, t) for c in al]
+        if a == "f":
+            return [("v" + b, t), ("b" + b, t), ("Y", t - 1)]
+        if a == "p":
+            return [("f" + str(int(b) // 2), t), ("Y", 1)]
+        if a == "q":
+            return [("r" + b, t)] + [("u" + c, t) for c in ("ab" if b == "0" else b)]
+
+    def call(x, t, k):
+        a, b = x[0], x[1:]
+        c = int(b) if b.isdigit() else None
+        vec = k == "v"
+        if a == "c":
+            return v.tensor_scalar(T.RA[:, C[c]], T.r0i[:, C[c]], -1.0, LAM, op.add, op.mult)
+        if x == "nb":
+            return v.tensor_copy(T.nbu[:], T.nbi[:])
+        if x == "lst":
+            for i in range(N - 1):
+                d = o[i] - 1
+                kk = fin(v.tensor_scalar(T.snf[:, 16 * i:16 * i + 16], T.sni[:, 16 * d:16 * d + 16], PAD - (CAP + 1) * BIG, None,
+                                         op.add), "vq")
+            need("v", kk)
+            return v.tensor_scalar(T.snu[:], T.snf[:], (CAP + 1) * BIG - PAD, None, op.add)
+        if a == "A":
+            if vec:
+                return v.tensor_scalar(T.AB[:, C[c]], R[t][:, C[c]], T.thc[:], 4.0, op.is_ge, op.mult)
+            return s.activation(T.AB[:, C[c]], R[t][:, C[c]], fn.Relu, bias=T.thb[:], scale=SC)
+        if a == "X":
+            return v.tensor_tensor(T.X[:, C[c]], R[t][:, C[c]], T.AB[:, C[c]], op.min)
+        if a == "W":
+            if vec:
+                return v.tensor_scalar(W[t][:, CW[c]], T.X[:, C[c]], Q4, 4.0, op.mult, op.add)
+            return s.activation(W[t][:, CW[c]], T.X[:, C[c]], fn.Identity, bias=4.0, scale=Q4)
+        if a == "G":
+            cs, cl = cols(*PARTS[c])
+            if vec:
+                return v.tensor_scalar(T.gs[:, cs], R[t][:, 0:V].indirect(T.snu[:, cl]), T.thc[:], None, op.is_ge)
+            return s.activation(T.gs[:, cs], R[t][:, 0:V].indirect(T.snu[:, cl]), fn.Relu, bias=T.thb[:], scale=SC)
+        if a == "P":
+            cs, cl = cols(*PARTS[c])
+            for i in range(16):
+                ins = pe.matmul(T.hot[:, cl], T.sel[:, 15 - i:143 - i], T.gs[:, cs.start + i:cs.stop:16], i == 0, i == 15)
+            return ins
+        if a == "H":
+            return v.tensor_scalar(T.hb[:], T.hot[:, HC], 0.0, None, op.is_gt)
+        if a == "C":
+            return v.tensor_tensor_scan(T.cs[:], T.rm[:], T.hb[:], 0.0, op.mult, op.add)
+        if a == "K":
+            pe.matmul(T.hot[:, YC], T.tri[:], T.hb[:], True, False)
+            return pe.matmul(T.hot[:, YC], T.blkn[:], T.cs[:], False, True)
+        if a == "Q":
+            return v.tensor_tensor(T.qf[:], T.snf[:], T.hot[:, YC], op.min)
+        if a == "L":
+            return v.tensor_scalar(T.lstu[:], T.qf[:], (CAP + 1) * BIG, 0.0, op.add, op.max)
+        if a == "M":
+            cs, cl = cols(*STAGES[c])
+            src = W[t][:, 0:PAD + V].indirect(T.lstu[:, cl])
+            if vec:
+                return v.tensor_copy(OB[t % 2][:, cs], src)
+            return s.activation(OB[t % 2][:, cs], src, fn.Identity)
+        if a == "d":
+            return v.tensor_tensor(T.AB[:, HF[c]], R[t][:, HF[c]], T.AB[:, HF[c]], op.subtract)
+        if a == "b":
+            if vec:
+                return v.tensor_scalar(T.AB[:, HF[c]], T.AB[:, HF[c]], LAM, 0.0, op.add, op.max)
+            return s.activation(T.AB[:, HF[c]], T.AB[:, HF[c]], fn.Relu, bias=LAM, scale=1.0)
+        if a == "e":
+            out = T.hot if t == RO - 1 else E[t % 2]
+            if vec:
+                return v.tensor_scalar(out[:, HF[c]], W[t][:, HW[c]], -2.0, 8.0, op.mult, op.add)
+            return s.activation(out[:, HF[c]], W[t][:, HW[c]], fn.Identity, bias=8.0, scale=-2.0)
+        if a in "tu":
+            i, n = PIECE[b]
+            cl = slice(i // 16, (i + n) // 16)
+            if a == "t":
+                return s.activation(T.TT[:, i:i + n], W[t][:, ALL].indirect(T.nbu[:, 128 + i // 16:128 + (i + n) // 16]),
+                                    fn.Identity, bias=-8.0, scale=ONE)
+            return v.tensor_tensor(U[t % 2][:, i:i + n], W[t][:, ALL].indirect(T.nbu[:, cl]), T.TT[:, i:i + n], op.add)
+        if a == "r":
+            return v.tensor_tensor(T.RB[:, C[c]], U[t % 2][:, C[c]], T.AB[:, C[c]], op.add)
+        if a == "v":
+            return v.tensor_tensor(T.X[:, HF[c]], T.RA[:, HF[c]], T.hot[:, HF[c]], op.add)
+        if a == "f":
+            return v.tensor_tensor(T.E0[:, HF[c]], T.X[:, HF[c]], T.AB[:, HF[c]], op.subtract)
+        if a == "p":
+            if vec:
+                return v.tensor_scalar(T.E1[:, C[c]], T.E0[:, C[c]], 1.0 / LAM, 4.0, op.mult, op.add)
+            return s.activation(T.E1[:, C[c]], T.E0[:, C[c]], fn.Identity, bias=4.0, scale=1.0 / LAM)
+        if a == "q":
+            if vec:
+                return v.tensor_scalar(T.TT[:, C[c]], T.RB[:, C[c]], 1.0 / LAM, 1.0, op.mult, op.add)
+            return s.activation(T.TT[:, C[c]], T.RB[:, C[c]], fn.Identity, bias=1.0, scale=1.0 / LAM)
+
+    todo = {k: [] for k in "vspgy"}
+
+    def put(part, t, tn=None):
+        for k in "vs":
+            for x in ORD[part][k]:
+                todo[k].append((x, t if tn is None or x[0] not in "AXWGHCQLM" else tn))
+
+    def slots(t):
+        for i in range(len(PARTS)):
+            todo["p"].append(("P%d" % i, t))
+        todo["p"].append(("K0", t))
+        for i in range(NST):
+            todo["g"].append(("S%d" % i, t))
+
+    put("start", 0)
+    todo["v"].insert(todo["v"].index(("X3", 0)), ("mat", 0))
+    tok["mat0"] = k4
+    slots(0)
+    for t in range(RO - 1):
+        put("wait", t)
+        todo["g"].append(("Y", t))
+        put("step", t, t + 1)
+        todo["g"].append(("Z", t))
+        slots(t + 1)
+    put("wait3", RO - 1)
+    put("end", RO - 1)
+    for x in OUT:
+        todo["y"].append(("o" + x, RO - 1))
+    for t in range(RO):
+        tok[("arr", t)] = ("arr%d" % t, arrive)
+    head = {k: 0 for k in todo}
+
+    def known(dp):
+        for x in dp:
+            if isinstance(x, tuple) and x[1] < 0:
+                if x[0][0] != "r":
+                    continue
+                x = "c" + x[0][1:]
+            elif isinstance(x, tuple) and x[0] == "left":
+                yield ("ls" + "ab"[x[1] % 2], left[x[1]]) if ("S%d" % (NST - 1), x[1]) in tok else "missing"
+                continue
+            yield tok.get(x, "missing")
+
+    more = True
+    while more:
+        more = False
+        for k in "vspgy":
+            while head[k] < len(todo[k]):
+                x, t = todo[k][head[k]]
+                got = list(known(deps(x, t) if k != "y" else [(x[1:], t)]))
+                if "missing" in got:
+                    break
+                need(k, *got)
+                nm = (x, t)
+                if x[0] == "S":
+                    send(int(x[1:]), t)
+                    tok[nm] = None
+                elif x == "mat":
+                    fin(v.tensor_scalar(T.blkn[:], T.bk2[:, 0:128], -BIG, None, op.mult), "vq")
+                    tok["mat"] = fin(v.tensor_scalar(T.tri[:], T.tri1[:], BIG, None, op.mult), "vq")
+                elif x[0] in "YZ":
+                    buf = E[t % 2] if x == "Y" else U[t % 2]
+                    tok[nm] = fin(g.dma_start(T.RA[:], buf[:], accum_op=op.add), "acc%d" % (2 * t + (x == "Z")), 16)
+                elif x[0] == "o":
+                    c = C[int(x[2:])]
+                    if x[1] == "p":
+                        fin(sy.dma_start(T.yp[:, c], T.E1[:, c]), "outp", 16)
+                    else:
+                        fin(sy.dma_start(T.yr[:, c], T.TT[:, c]), "outr", 16)
+                    tok[nm] = None
+                else:
+                    tok[nm] = fin(call(x, t, k), {"v": "vq", "s": "sq", "p": "pq"}[k])
+                    if x[0] == "c" or x in ("nb", "lst"):
+                        tok[x] = tok[nm]
+                head[k] += 1
+                more = True
+    assert all(head[k] == len(todo[k]) for k in todo), [(k, todo[k][head[k]]) for k in todo if head[k] < len(todo[k])]
+    need("y", ("outp", cnt["outp"]), ("outr", cnt["outr"]))
+    for name in ("vq", "sq", "pq", "gq", "lsa", "lsb"):
+        need("g", (name, cnt[name]))

@@ -7,32 +7,48 @@ NS = (N - 1) * G
 NC = NS // 16
 PAD = 8
 BIG = 4096.0
+MAG = 2.0 ** 23
+Q4 = 0.25 * (1.0 - 2.0 ** -23)
+CH = 512
+NCH = V // CH
+NB = 7
 SCRATCH = {
     "r0i": ("sbuf", [128, V], "int32"),
     "thi": ("sbuf", [128, 1], "int32"),
     "thb": ("sbuf", [128, 1], "float32"),
+    "thf": ("sbuf", [128, 1], "float32"),
     "thc": ("sbuf", [128, 1], "float32"),
     "nbi": ("sbuf", [128, 256], "int32"),
     "nbu": ("sbuf", [128, 256], "uint16"),
     "sni": ("sbuf", [128, NC], "int32"),
+    "snh": ("sbuf", [128, NC + 32], "float16"),
+    "tr0": ("sbuf", [128, 128], "float16"),
+    "tr1": ("sbuf", [128, 128], "float16"),
     "snf": ("sbuf", [128, NC], "float32"),
     "snu": ("sbuf", [128, NC], "uint16"),
     "qf": ("sbuf", [128, NC], "float32"),
     "lstu": ("sbuf", [128, NC], "uint16"),
-    "one": ("sbuf", [128, 144], "bfloat16"),
+    "big": ("sbuf", [128, 144], "bfloat16"),
+    "zb": ("sbuf", [128, CH], "bfloat16"),
+    "zf": ("sbuf", [128, 128], "float32"),
     "bk1": ("sbuf", [128, 144], "bfloat16"),
     "bk2": ("sbuf", [128, 144], "bfloat16"),
     "sel": ("sbuf", [128, 144], "bfloat16"),
-    "tri1": ("sbuf", [128, 128], "bfloat16"),
     "tri": ("sbuf", [128, 128], "bfloat16"),
-    "blkn": ("sbuf", [128, 128], "bfloat16"),
+    "up": ("sbuf", [128, 128], "bfloat16"),
+    "par0": ("sbuf", [128, 128], "bfloat16"),
+    "par1": ("sbuf", [128, 128], "bfloat16"),
+    "low": ("sbuf", [128, 128], "bfloat16"),
+    "down": ("sbuf", [128, 128], "bfloat16"),
+    "id1": ("sbuf", [128, 128], "float32"),
+    "col": ("sbuf", [128, NC], "float32"),
     "rm": ("sbuf", [128, NC], "bfloat16"),
     "hb": ("sbuf", [128, NC], "bfloat16"),
     "cs": ("sbuf", [128, NC], "bfloat16"),
-    "RA": ("sbuf", [128, V], "float32"),
-    "RB": ("sbuf", [128, V], "float32"),
-    "X": ("sbuf", [128, V], "float32"),
+    "F": ("sbuf", [128, V], "bfloat16"),
+    "X": ("sbuf", [128, PAD + V], "float32"),
     "TT": ("sbuf", [128, V], "float32"),
+    "RA": ("sbuf", [128, V], "float32"),
     "U0": ("sbuf", [128, V], "float32"),
     "U1": ("sbuf", [128, V], "float32"),
     "E0": ("sbuf", [128, V], "float32"),
@@ -40,30 +56,37 @@ SCRATCH = {
     "gs": ("sbuf", [128, NS], "bfloat16"),
     "ob0": ("sbuf", [128, NS], "float32"),
     "ob1": ("sbuf", [128, NS], "float32"),
-    "W0": ("sbuf", [128, PAD + V + NS], "float32"),
-    "W1": ("sbuf", [128, PAD + V + NS], "float32"),
-    "W2": ("sbuf", [128, PAD + V + NS], "float32"),
-    "W3": ("sbuf", [128, PAD + V + NS], "float32"),
-    "AB": ("psum", [128, V], "float32"),
-    "hot": ("psum", [128, V], "float32"),
+    "W0": ("sbuf", [128, V + NS], "float32"),
+    "W1": ("sbuf", [128, V + NS], "float32"),
+    "W2": ("sbuf", [128, V + NS], "float32"),
+    "W3": ("sbuf", [128, V + NS], "float32"),
+    "R": ("psum", [128, CH * NB], "float32"),
+    "hot": ("psum", [128, CH], "float32"),
 }
-SEMAPHORES = (["vq", "sq", "pq", "gq", "lsa", "lsb", "lth", "lsn", "lnb", "outp", "outr"] + ["lr%d" % c for c in range(4)]
+SEMAPHORES = (["vq", "sq", "pq", "gq", "lsa", "lsb", "lth", "lsn", "lnb", "outr"] + ["lr%d" % c for c in range(NCH)]
               + ["arr%d" % t for t in range(RO)] + ["acc%d" % k for k in range(2 * RO)])
 
-STAGES = ((0, 1), (1, 2), (3, 2), (5, 2))
-PARTS = ((0, 3), (3, 4))
+STAGES = ((1,), (2, 2), (2, 2), (2, 2))
+MP = ((0, 256), (256, 512), (768, 512), (1280, 512))
+LOW = 2.0 ** 22
+PARTS = ((0, 6), (6, 4), (10, 4), (14, 2))
+PIECE = {"a": (0, 256), "b": (256, 256), "1": (512, 512), "2": (1024, 512), "3": (1536, 512)}
 
 ORD = {
-    "start": {"v": "c0 c1 lst c2 c3 G0 X0 X1 X2 X3 H0 C0 Q0 L0 M1 M3 nb".split(),
-              "s": "A0 A1 A2 A3 G1 W0 W1 W2 W3 M0 M2".split()},
-    "step": {"v": "ub ua r0 u1 u2 r1 u3 r2 r3 G0 X0 X1 X2 X3 H0 C0 Q0 L0 M1 M3".split(),
-             "s": "tb ta t1 t2 t3 A0 A1 A2 A3 G1 W0 W1 W2 W3 M0 M2".split()},
-    "wait": {"v": "d1 d0 b0".split(), "s": "e1 e0 b1".split()},
-    "wait3": {"v": "d1 d0 v1 v0 f1 f0".split(), "s": "e0 e1 b1 b0".split()},
-    "end": {"v": "ua ub u1 r0 u2 r1 r2 u3 r3 p3".split(),
-            "s": "ta tb t1 t2 p0 p1 t3 q0 q1 p2 q2 q3".split()},
+    "first": {"v": "c0 sh c1 c2 c3 su B3 sf G0 X0 X1 X2 C0 X3 Q0 L0 M1 M3 b1 b2 nb b0 i0 i1 b3 i2 i3".split(),
+              "s": "A0 A1 A2 G1 G2 G3 W0 H0 e0 W1 M0 M2 W3 W2 e2 e1 e3".split(),
+              "p": "z1 z2 sp z0 P1 P0 P2 P3 K0 n1 n2 z3 n0 n3".split()},
+    "mid": {"v": "tb ua ub u1 u2 r1 u3 r2 r3 X0 G0 X3 X2 H0 C0 X1 Q0 L0 M1 M3 b0 b2 b3 b1 D3 D2".split(),
+            "s": "ta t1 t2 t3 A1 A0 A2 A3 G1 G2 G3 W3 W2 W0 M0 M2 W1 e2 e3 e1 e0".split(),
+            "p": "a0 z1 z0 z2 P1 P0 P2 P3 K0 z3 n0 n3 n1 n2".split()},
+    "last": {"v": "tb ua ub u1 u2 r1 u3 r2 r3 X0 G0 X1 X2 H0 C0 X3 Q0 L0 M1 M3 b0 b1 b2 b3 N0 N2 N3 N1".split(),
+             "s": "ta t1 t2 t3 A1 A0 A2 A3 G1 G2 G3 W0 W2 e0 M0 M2 W3 e2 W1 e3 e1 k1".split(),
+             "p": "a0 z2 z0 z1 P1 P0 P2 P3 K0 z3 n0 n1 y1 n2 n3".split()},
+    "end": {"v": "u1 u2 ua r2 ub u3 r0 r3".split(),
+            "s": "t1 t2 ta tb t3 q1".split(),
+            "p": "a1".split()},
 }
-OUT = "p0 p1 q0 q1 p2 q2 p3 q3".split()
+OUT = "r2 q1 r0 r3".split()
 
 
 def order(q, T, topo):
@@ -80,11 +103,14 @@ def order(q, T, topo):
 
 
 def lanes(q, T, topo):
-    o, res = order(q, T, topo), {}
-    for first, n in STAGES:
-        for k in range(n):
-            e = topo.engines(T.cores[q], T.cores[(q + o[first + k]) % N])
-            res[o[first + k]] = e[k::n]
+    o, res = iter(order(q, T, topo)), {}
+    for stage in STAGES:
+        used = []
+        for n in stage:
+            d = next(o)
+            e = topo.engines(T.cores[q], T.cores[(q + d) % N])
+            res[d] = next(e[k::n] for k in range(n) if e[k] not in used)
+            used += res[d]
     return res
 
 
@@ -96,11 +122,7 @@ def rank_program(g, core, T, topo):
     eng = {"g": g, "v": v, "s": s, "p": pe, "y": sy}
     cnt, seen, tok = {}, {}, {}
     op, fn = AluOpType, ActivationFunctionType
-    LAM = 2.0 ** -21
-    SC = 2.0 ** 22
-    ONE = 1.0 - 2.0 ** -23
-    Q4 = 0.25 * ONE
-    NST = len(STAGES)
+    NST, LAST = len(STAGES), RO - 1
 
     def need(k, *toks):
         for name, val in toks:
@@ -115,23 +137,38 @@ def rank_program(g, core, T, topo):
 
     o, lane = order(q, T, topo), lanes(q, T, topo)
     arrive = sum(len(lanes((q - d) % N, T, topo)[d]) for d in range(1, N))
-    C = [slice(512 * c, 512 * c + 512) for c in range(4)]
-    CW = [slice(PAD + 512 * c, PAD + 512 * c + 512) for c in range(4)]
-    HF = [slice(1024 * h, 1024 * h + 1024) for h in range(2)]
-    HW = [slice(PAD + 1024 * h, PAD + 1024 * h + 1024) for h in range(2)]
-    ALL = slice(PAD, PAD + V + NS)
+    C = [slice(CH * c, CH * (c + 1)) for c in range(NCH)]
+    CX = [slice(PAD + CH * c, PAD + CH * (c + 1)) for c in range(NCH)]
     W = [T["W%d" % t] for t in range(RO)]
     U, E, OB = [T.U0, T.U1], [T.E0, T.E1], [T.ob0, T.ob1]
-    R = [T.RA, T.RB, T.RB, T.RB, T.RB]
-    PIECE = {"a": (0, 256), "b": (256, 256), "1": (512, 512), "2": (1024, 512), "3": (1536, 512)}
-    HC, YC = slice(0, NC), slice(512, 512 + NC)
+    HC, YC = slice(0, NC), slice(128, 128 + NC)
     left = {}
 
-    def cols(a, n):
-        return slice(G * a, G * (a + n)), slice(16 * a, 16 * (a + n))
+    def part(t):
+        return ORD[("first", "mid", "mid", "last", "end")[t]]
+
+    def res(c, t):
+        k = (NCH * t + c) % NB
+        return T.R[:, CH * k:CH * (k + 1)]
+
+    def before(c, t):
+        k = NCH * t + c - NB
+        return (str(k % NCH), k // NCH)
+
+    def pieces(b):
+        return [x for x in PIECE if PIECE[x][0] // CH == int(b)]
+
+    def added(b, t):
+        return "a" + b in part(t + 1)["p"]
+
+    def joined(b, t):
+        return t >= 0 and "D" + b in part(t)["v"]
+
+    def alone(t):
+        return CH * sum(not joined(str(c), t + 1) for c in range(NCH))
 
     def send(i, t):
-        a, n = STAGES[i]
+        a, n = sum(map(len, STAGES[:i])), len(STAGES[i])
         ls = "ls" + "ab"[t % 2]
         tr = []
         for k in range(n):
@@ -140,7 +177,7 @@ def rank_program(g, core, T, topo):
             ad = topo.addr(dst)
             m = sum(1 << e for e in lane[d])
             src = OB[t % 2][:, G * (a + k):G * (a + k + 1)]
-            out = W[t][:, PAD + V + (d - 1) * G:PAD + V + d * G]
+            out = W[t][:, V + (d - 1) * G:V + d * G]
             cnt[ls] = cnt.get(ls, 0) + len(lane[d])
             if n == 1:
                 g.remote_dma(out, src, T.sem["arr%d" % t], T.sem[ls], ad[1], ad[0], m)
@@ -152,203 +189,240 @@ def rank_program(g, core, T, topo):
         left[t] = cnt[ls]
 
     tok["th"] = fin(s.dma_start(T.thi[:], T.th[:]), "lth", 16)
-    for c in range(4):
-        tok["l%d" % c] = fin(sy.dma_start(T.r0i[:, C[c]], T.r0[:, C[c]]), "lr%d" % c, 16)
     tok["sn"] = fin(s.dma_start(T.sni[:], T.snd[:]), "lsn", 16)
-    tok["nbl"] = fin(s.dma_start(T.nbi[:], T.nb[:]), "lnb", 16)
-    k1 = fin(v.memset(T.one[:], 1.0), "vq")
+    for c in range(NCH):
+        tok["l%d" % c] = fin(sy.dma_start(T.r0i[:, C[c]], T.r0[:, C[c]]), "lr%d" % c, 16)
+    tok["nbl"] = fin(sy.dma_start(T.nbi[:], T.nb[:]), "lnb", 16)
+    k0 = fin(g.iota(T.col[:], [[0, N - 1], [1, 16]], 0, 0, allow_small_or_imprecise_dtypes=True), "gq")
+    need("s", k0)
+    tok["rm"] = fin(s.activation(T.rm[:], T.col[:], fn.Sigmoid, bias=-128.0, scale=256.0), "sq")
+    tok["zb"] = fin(v.memset(T.zb[:], 0.0), "vq")
+    kb = fin(v.memset(T.big[:], BIG), "vq")
+    kf = fin(v.memset(T.zf[:], 0.0), "vq")
+    tok["pad"] = fin(v.memset(T.X[:, 0:PAD], 0.0), "vq")
+    need("v", tok["zb"])
+    tok["zh"] = fin(v.tensor_copy(T.snh[:], T.zb[:, 0:NC + 32]), "vq")
+
+    def diag(out, zero, x):
+        return fin(g.affine_select(out[:], zero[:, 0:128], [[-1, 128]], op.not_equal, x, 0, 1), "gq")
+
+    need("g", tok["zb"])
+    k1 = diag(T.up, T.zb, 1.0)
     need("g", k1)
-    k2 = fin(g.affine_select(T.bk1[:], T.one[:], [[-16, 9], [0, 16]], op.is_ge, 0.0, 0, 1), "gq")
-    tok["rm"] = fin(g.affine_select(T.rm[:], T.one[:, 0:NC], [[0, N - 1], [1, 16]], op.is_gt, 0.0, 0, 0), "gq")
+    for k, par in enumerate((T.par0, T.par1)):
+        tok["par"] = fin(g.affine_select(par[:], T.up[:], [[0, 4], [1, 2], [0, 16]], op.is_equal, 0.0, -k, 0), "gq")
+    need("g", kb)
+    k2 = fin(g.affine_select(T.bk1[:], T.big[:], [[-16, 9], [0, 16]], op.is_ge, 0.0, 0, 1), "gq")
     need("g", k2)
     k3 = fin(g.affine_select(T.bk2[:], T.bk1[:], [[16, 9], [0, 16]], op.is_ge, 0.0, 15, -1), "gq")
     need("g", k3)
     tok["sel"] = fin(g.affine_select(T.sel[:], T.bk2[:], [[0, 9], [1, 16]], op.is_equal, 0.0, -15, 0), "gq")
-    k4 = fin(g.affine_select(T.tri1[:], T.bk2[:, 0:128], [[-1, 128]], op.is_gt, 0.0, 0, 1), "gq")
-    for t in range(RO):
-        tok["pad"] = fin(v.memset(W[t][:, 0:PAD], 4.0), "vq")
+    tok["tri"] = fin(g.affine_select(T.tri[:], T.bk2[:, 0:128], [[-1, 128]], op.is_gt, 0.0, 0, 1), "gq")
+    need("g", kf)
+    tok["down"] = diag(T.down, T.zb, -1.0)
+    tok["id1"] = diag(T.id1, T.zf, 1.0)
     need("v", tok["th"])
-    tok["thb"] = fin(v.tensor_scalar(T.thb[:], T.thi[:], -2.0, 4.0, op.mult, op.add), "vq")
-    tok["thc"] = fin(v.tensor_scalar(T.thc[:], T.thi[:], -1.0, LAM, op.add, op.mult), "vq")
+    tok["thb"] = fin(v.tensor_scalar(T.thb[:], T.thi[:], -256.0, 384.0, op.mult, op.add), "vq")
+    tok["thf"] = fin(v.tensor_copy(T.thf[:], T.thi[:]), "vq")
+    tok["thc"] = fin(v.tensor_scalar(T.thc[:], T.thi[:], -1.0, None, op.add), "vq")
+
+    al = [str(c) for c in range(NCH)]
+    gp = [str(i) for i in range(len(PARTS))]
+    st = [str(i) for i in range(len(MP))]
 
     def deps(x, t):
         a, b = x[0], x[1:]
-        al = ["0", "1", "2", "3"]
-        gp = [str(i) for i in range(len(PARTS))]
-        st = [str(i) for i in range(NST)]
         if a == "c":
             return ["l" + b]
         if x == "nb":
             return ["nbl"]
-        if x == "mat":
-            return ["mat0"]
-        if x == "lst":
-            return ["sn"]
-        if a == "A":
-            return ["thb", "thc", ("r" + b, t - 1)]
+        if a == "s":
+            return {"h": ["sn", "zh"], "p": ["par", "sh"], "u": ["sp"], "f": ["sp"]}[b]
+        if a in "Ah":
+            whole = "c" + b if t == 0 else ("a" + b if added(b, t - 1) else "r" + b, t - 1)
+            if a == "h":
+                return [whole, ("j" + b, t)] + [("A" + b, t)] * ("A" + b in part(t)["v"])
+            return ["thb", "thc", whole, ("n" + b, t - 1), ("X" + b, t - 1)] + [("G" + i, t - 1) for i in gp]
+        if a == "l":
+            return ["low", ("h" + b, t), ("A" + b, t)]
         if a == "X":
-            return [("A" + b, t), ("r" + b, t - 1), ("W" + b, t - 1)]
+            return ([("A" + b, t), "c" + b, ("W" + b, t - 1), ("b" + b, t - 1)] + [("M" + i, t - 1) for i in st]
+                    + [("l" + b, t)] * ("l" + b in part(t)["p"]))
         if a == "W":
             return [("X" + b, t)]
+        if a in "zj":
+            pb, pt = before(int(b), t + 1)
+            if a == "z" and "l" + b in part(t)["p"]:
+                return [("X" + b, t)]
+            return ["zb", ("b" + pb, pt)] + [("i" + pb, pt)] * (pt == 0) + [("D" + pb, pt)] * joined(pb, pt)
+        if a == "b":
+            return [("z" + b, t), ("X" + b, t)]
+        if a == "n":
+            return ["down", ("b" + b, t)]
+        if a == "i":
+            return [("b" + b, t), ("e" + b, t)]
+        if a == "e":
+            return [("W" + b, t), ("b" + b, t) if joined(b, t) else ("Y", t - 2) if t > 2 else ("i" + b, t - 2)]
+        if a == "D":
+            return [("e" + b, t), ("i" + b, t - 2)]
+        if a == "N":
+            return [("e" + b, t), ("n" + b, t), ("Y", t - 1)] + [("k" + b, t)] * added(b, t)
+        if a == "y":
+            return [("b" + b, t)]
+        if a == "k":
+            return [("y" + b, t), ("n" + b, t)]
+        if a == "q":
+            return [("a" + b, t)]
+        if a == "B":
+            return ["thf", "l" + b]
+        if a == "I":
+            return [("i" + c, t) for c in al]
+        if a == "Y":
+            return ([(("N" if t == LAST else "D" if joined(c, t) else "e") + c, t) for c in al]
+                    + [("Z", t - 1) if alone(t - 1) else ("Y" if t > 1 else "I", t - 1)])
+        if a == "Z":
+            return [("u" + c, t) for c in PIECE] + [("Y" if t else "I", t)]
         if a == "G":
-            return ["thb", "thc", "lst"] + [("r" + c, t - 1) for c in al] + [("P" + b, t - 1)]
+            return ["su"] + [("A" + c, t) for c in al] + [("P" + b, t - 1)]
         if a == "P":
-            return ["sel", ("G" + b, t), ("H0", t - 1)]
+            return ["sel", "su", "sf", ("G" + b, t), ("Q0", t - 1)]
         if a == "H":
             return [("P" + i, t) for i in gp] + [("C0", t - 1), ("K0", t - 1)]
         if a == "C":
             return ["rm", ("H0", t), ("K0", t - 1)]
         if a == "K":
-            return ["mat", ("C0", t), ("Q0", t - 1)]
+            return ["tri", ("C0", t)]
         if a == "Q":
             return [("K0", t), ("L0", t - 1)]
         if a == "L":
             return [("Q0", t)] + [("M" + i, t - 1) for i in st]
         if a == "M":
-            return ["pad", ("L0", t)] + [("W" + c, t) for c in al] + [("left", t - 2)]
+            return ["pad", ("L0", t)] + [("X" + c, t) for c in al] + [("left", t - 2)]
         if a == "S":
-            return [("M" + b, t)]
-        if a == "d":
-            return [("X" + str(2 * int(b) + h), t) for h in range(2)]
-        if a == "b":
-            return [("d" + b, t)]
-        if a == "e":
-            w2 = [("W" + c, t) for c in (al[:2] if b == "0" else al[2:])]
-            if t == RO - 1:
-                return w2 + [("Q0", t)]
-            return w2 + [("Y", t - 2)]
-        if a == "Y":
-            return [("e0", t), ("e1", t), ("d0", t), ("d1", t), ("Z", t - 1)] + [("G" + i, t) for i in gp]
-        if a == "Z":
-            return [("Y", t)] + [("u" + c, t) for c in "ab123"]
+            lo = G * sum(map(len, STAGES[:int(b)]))
+            hi = lo + G * len(STAGES[int(b)])
+            return [("M%d" % i, t) for i, (at, n) in enumerate(MP) if at < hi and at + n > lo]
         if a == "t":
             return ["nb", ("arr", t)] + [("W" + c, t) for c in al] + [("u" + b, t - 1)]
         if a == "u":
-            return ["nb", ("arr", t)] + [("W" + c, t) for c in al] + [("t" + b, t), ("Z", t - 2)]
+            c = str(PIECE[b][0] // CH)
+            return (["nb", ("arr", t)] + [("W" + c, t) for c in al]
+                    + [("t" + b, t), ("D" + c, t - 1) if joined(c, t - 1) else ("Z", t - 2),
+                       (("a" if added(c, t - 2) else "r") + c, t - 2)])
+        if a == "a":
+            return ["id1", ("k" + b if t == LAST else "n" + b, t)] + [("u" + i, t) for i in pieces(b)]
         if a == "r":
-            return [("b" + str(int(b) // 2), t)] + [("u" + c, t) for c in ("ab" if b == "0" else b)]
-        if a == "v":
-            return [("e" + b, t), ("Z", t - 1)] + [("W" + c, t) for c in al]
-        if a == "f":
-            return [("v" + b, t), ("b" + b, t), ("Y", t - 1)]
-        if a == "p":
-            return [("f" + str(int(b) // 2), t), ("Y", 1)]
-        if a == "q":
-            return [("r" + b, t)] + [("u" + c, t) for c in ("ab" if b == "0" else b)]
+            return [("n" + b, t)] + [("u" + i, t) for i in pieces(b)]
+
+    def affine(k, out, src, scale, bias):
+        if k == "s":
+            return s.activation(out, src, fn.Identity, bias=bias, scale=scale)
+        return v.tensor_scalar(out, src, scale, bias, op.mult, op.add)
 
     def call(x, t, k):
         a, b = x[0], x[1:]
         c = int(b) if b.isdigit() else None
         vec = k == "v"
         if a == "c":
-            return v.tensor_scalar(T.RA[:, C[c]], T.r0i[:, C[c]], -1.0, LAM, op.add, op.mult)
+            return v.tensor_scalar(res(c, 0), T.r0i[:, C[c]], -1.0, None, op.add)
         if x == "nb":
             return v.tensor_copy(T.nbu[:], T.nbi[:])
-        if x == "lst":
+        if x == "sh":
+            need("v", fin(v.tensor_copy(T.snh[:, 16:16 + NC], T.sni[:]), "vq"))
+            fin(v.transpose(T.tr0[:], T.snh[:, 16:144]), "vq")
+            return v.transpose(T.tr1[:], T.snh[:, 0:128])
+        if x == "sp":
             for i in range(N - 1):
                 d = o[i] - 1
-                kk = fin(v.tensor_scalar(T.snf[:, 16 * i:16 * i + 16], T.sni[:, 16 * d:16 * d + 16], PAD - (CAP + 1) * BIG, None,
-                                         op.add), "vq")
-            need("v", kk)
-            return v.tensor_scalar(T.snu[:], T.snf[:], (CAP + 1) * BIG - PAD, None, op.add)
+                for par in range(2):
+                    at = 16 * d if d % 2 == par else 16 * (d + 1)
+                    pe.matmul(T.hot[:, i:NC:N - 1], (T.par0, T.par1)[par][:], (T.tr0 if d % 2 == par else T.tr1)[:, at:at + 16],
+                              par == 0, par == 1)
+                ins = pe.matmul(T.hot[:, 128 + 16 * i:144 + 16 * i], T.up[:], T.snh[:, 16 + 16 * d:32 + 16 * d], True, True)
+            return ins
+        if x == "su":
+            return v.tensor_copy(T.snu[:], T.hot[:, HC])
+        if x == "sf":
+            return v.tensor_scalar(T.snf[:], T.hot[:, YC], PAD - (CAP + 1) * BIG, None, op.add)
         if a == "A":
             if vec:
-                return v.tensor_scalar(T.AB[:, C[c]], R[t][:, C[c]], T.thc[:], 4.0, op.is_ge, op.mult)
-            return s.activation(T.AB[:, C[c]], R[t][:, C[c]], fn.Relu, bias=T.thb[:], scale=SC)
+                return v.tensor_scalar(T.F[:, C[c]], res(c, t), T.thc[:], None, op.is_ge)
+            return s.activation(T.F[:, C[c]], res(c, t), fn.Sigmoid, bias=T.thb[:], scale=256.0)
+        if a == "h":
+            return affine(k, res(c, t + 1), res(c, t), 1.0, -LOW)
+        if a == "l":
+            return pe.matmul(res(c, t + 1), T.low[:], T.F[:, C[c]], False, True)
         if a == "X":
-            return v.tensor_tensor(T.X[:, C[c]], R[t][:, C[c]], T.AB[:, C[c]], op.min)
+            if vec:
+                return v.tensor_tensor(T.X[:, CX[c]], res(c, t), T.F[:, C[c]], op.mult)
+            return s.activation(T.X[:, CX[c]], res(c, t + 1), fn.Relu)
         if a == "W":
-            if vec:
-                return v.tensor_scalar(W[t][:, CW[c]], T.X[:, C[c]], Q4, 4.0, op.mult, op.add)
-            return s.activation(W[t][:, CW[c]], T.X[:, C[c]], fn.Identity, bias=4.0, scale=Q4)
+            return affine(k, W[t][:, C[c]], T.X[:, CX[c]], Q4, MAG)
+        if a in "zjy":
+            return pe.matmul(res(c, t + (a != "y")), T.zb[:, 0:128], T.zb[:], True, False)
+        if a == "k":
+            return affine(k, res(c, t), res(c, t + 1), 1.0, 0.0)
+        if a == "q":
+            return affine(k, T.W1[:, C[c]], res(c, t), 1.0, 0.0)
+        if a == "B":
+            return v.tensor_scalar(T.F[:, C[c]], T.r0i[:, C[c]], T.thf[:], None, op.is_ge)
+        if a == "b":
+            return v.tensor_tensor(res(c, t + 1), res(c, t), T.X[:, CX[c]], op.subtract)
+        if a == "n":
+            return pe.matmul(res(c, t + 1), T.down[:], T.F[:, C[c]], False, t == LAST or not added(b, t))
+        if a == "a":
+            return pe.matmul(res(c, t + (t < LAST)), T.id1[:], U[t % 2][:, C[c]], False, True)
+        if a == "r":
+            out = T.W1[:, C[c]] if t == LAST else res(c, t + 1)
+            return v.tensor_tensor(out, U[t % 2][:, C[c]], res(c, t + 1), op.add)
         if a == "G":
-            cs, cl = cols(*PARTS[c])
-            if vec:
-                return v.tensor_scalar(T.gs[:, cs], R[t][:, 0:V].indirect(T.snu[:, cl]), T.thc[:], None, op.is_ge)
-            return s.activation(T.gs[:, cs], R[t][:, 0:V].indirect(T.snu[:, cl]), fn.Relu, bias=T.thb[:], scale=SC)
+            i, n = PARTS[c]
+            out, src = T.gs[:, NC * i:NC * (i + n)], T.F[:, 0:V].indirect(T.snu[:, (N - 1) * i:(N - 1) * (i + n)])
+            return v.tensor_copy(out, src) if vec else s.activation(out, src, fn.Identity)
         if a == "P":
-            cs, cl = cols(*PARTS[c])
-            for i in range(16):
-                ins = pe.matmul(T.hot[:, cl], T.sel[:, 15 - i:143 - i], T.gs[:, cs.start + i:cs.stop:16], i == 0, i == 15)
+            i, n = PARTS[c]
+            turn = [y for y in part(t)["p"] if y[0] == "P"]
+            for j in range(i, i + n):
+                ins = pe.matmul(T.hot[:, HC], T.sel[:, 15 - j:143 - j], T.gs[:, NC * j:NC * (j + 1)],
+                                j == i and x == turn[0], j == i + n - 1 and x == turn[-1])
             return ins
         if a == "H":
-            return v.tensor_scalar(T.hb[:], T.hot[:, HC], 0.0, None, op.is_gt)
+            return v.tensor_scalar(T.hb[:], T.hot[:, HC], 0.0, None, op.is_gt) if vec else s.activation(T.hb[:], T.hot[:, HC], fn.Sign)
         if a == "C":
-            return v.tensor_tensor_scan(T.cs[:], T.rm[:], T.hb[:], 0.0, op.mult, op.add)
+            return v.tensor_tensor_scan(T.cs[:], T.rm[:], T.hb[:], 0.0, op.mult, op.subtract)
         if a == "K":
             pe.matmul(T.hot[:, YC], T.tri[:], T.hb[:], True, False)
-            return pe.matmul(T.hot[:, YC], T.blkn[:], T.cs[:], False, True)
+            return pe.matmul(T.hot[:, YC], T.bk2[:, 0:128], T.cs[:], False, True)
         if a == "Q":
             return v.tensor_tensor(T.qf[:], T.snf[:], T.hot[:, YC], op.min)
         if a == "L":
             return v.tensor_scalar(T.lstu[:], T.qf[:], (CAP + 1) * BIG, 0.0, op.add, op.max)
         if a == "M":
-            cs, cl = cols(*STAGES[c])
-            src = W[t][:, 0:PAD + V].indirect(T.lstu[:, cl])
-            if vec:
-                return v.tensor_copy(OB[t % 2][:, cs], src)
-            return s.activation(OB[t % 2][:, cs], src, fn.Identity)
-        if a == "d":
-            return v.tensor_tensor(T.AB[:, HF[c]], R[t][:, HF[c]], T.AB[:, HF[c]], op.subtract)
-        if a == "b":
-            if vec:
-                return v.tensor_scalar(T.AB[:, HF[c]], T.AB[:, HF[c]], LAM, 0.0, op.add, op.max)
-            return s.activation(T.AB[:, HF[c]], T.AB[:, HF[c]], fn.Relu, bias=LAM, scale=1.0)
+            i, n = MP[c]
+            return affine(k, OB[t % 2][:, i:i + n], T.X[:, 0:PAD + V].indirect(T.lstu[:, i // 16:(i + n) // 16]), Q4, MAG)
+        if a == "i":
+            return v.tensor_tensor(T.RA[:, C[c]], res(c, 0), T.E0[:, C[c]], op.add)
         if a == "e":
-            out = T.hot if t == RO - 1 else E[t % 2]
-            if vec:
-                return v.tensor_scalar(out[:, HF[c]], W[t][:, HW[c]], -2.0, 8.0, op.mult, op.add)
-            return s.activation(out[:, HF[c]], W[t][:, HW[c]], fn.Identity, bias=8.0, scale=-2.0)
+            return affine(k, res(c, t) if joined(b, t) else E[t % 2][:, C[c]], W[t][:, C[c]], -2.0, 2.0 * MAG)
+        if a == "D":
+            return v.tensor_tensor(E[t % 2][:, C[c]], res(c, t), U[(t - 1) % 2][:, C[c]], op.add)
+        if a == "N":
+            return v.tensor_tensor(T.E0[:, C[c]], T.E1[:, C[c]], res(c, t + 1), op.subtract)
         if a in "tu":
             i, n = PIECE[b]
-            cl = slice(i // 16, (i + n) // 16)
+            cs, i, n = slice(i, i + n), i // 16, n // 16
             if a == "t":
-                return s.activation(T.TT[:, i:i + n], W[t][:, ALL].indirect(T.nbu[:, 128 + i // 16:128 + (i + n) // 16]),
-                                    fn.Identity, bias=-8.0, scale=ONE)
-            return v.tensor_tensor(U[t % 2][:, i:i + n], W[t][:, ALL].indirect(T.nbu[:, cl]), T.TT[:, i:i + n], op.add)
-        if a == "r":
-            return v.tensor_tensor(T.RB[:, C[c]], U[t % 2][:, C[c]], T.AB[:, C[c]], op.add)
-        if a == "v":
-            return v.tensor_tensor(T.X[:, HF[c]], T.RA[:, HF[c]], T.hot[:, HF[c]], op.add)
-        if a == "f":
-            return v.tensor_tensor(T.E0[:, HF[c]], T.X[:, HF[c]], T.AB[:, HF[c]], op.subtract)
-        if a == "p":
-            if vec:
-                return v.tensor_scalar(T.E1[:, C[c]], T.E0[:, C[c]], 1.0 / LAM, 4.0, op.mult, op.add)
-            return s.activation(T.E1[:, C[c]], T.E0[:, C[c]], fn.Identity, bias=4.0, scale=1.0 / LAM)
-        if a == "q":
-            if vec:
-                return v.tensor_scalar(T.TT[:, C[c]], T.RB[:, C[c]], 1.0 / LAM, 1.0, op.mult, op.add)
-            return s.activation(T.TT[:, C[c]], T.RB[:, C[c]], fn.Identity, bias=1.0, scale=1.0 / LAM)
+                return affine(k, T.TT[:, cs], W[t][:, 0:V + NS].indirect(T.nbu[:, 128 + i:128 + i + n]), 1.0,
+                              (t == LAST) - 2.0 * MAG)
+            return v.tensor_tensor(U[t % 2][:, cs], W[t][:, 0:V + NS].indirect(T.nbu[:, i:i + n]), T.TT[:, cs], op.add)
 
     todo = {k: [] for k in "vspgy"}
-
-    def put(part, t, tn=None):
-        for k in "vs":
-            for x in ORD[part][k]:
-                todo[k].append((x, t if tn is None or x[0] not in "AXWGHCQLM" else tn))
-
-    def slots(t):
-        for i in range(len(PARTS)):
-            todo["p"].append(("P%d" % i, t))
-        todo["p"].append(("K0", t))
-        for i in range(NST):
-            todo["g"].append(("S%d" % i, t))
-
-    put("start", 0)
-    todo["v"].insert(todo["v"].index(("X3", 0)), ("mat", 0))
-    tok["mat0"] = k4
-    slots(0)
-    for t in range(RO - 1):
-        put("wait", t)
-        todo["g"].append(("Y", t))
-        put("step", t, t + 1)
-        todo["g"].append(("Z", t))
-        slots(t + 1)
-    put("wait3", RO - 1)
-    put("end", RO - 1)
-    for x in OUT:
-        todo["y"].append(("o" + x, RO - 1))
+    for t in range(RO + 1):
+        for k in "vsp":
+            todo[k] += [(x, t - 1 if x[0] in "tuar" or t == RO else t) for x in part(t)[k]]
+    for t in range(RO):
+        todo["g"] += [("Z", t - 1)] * (t > 0 and alone(t - 1) > 0) + [("S%d" % i, t) for i in range(NST)] + [("Y", t)] * (t > 0)
+    todo["y"] += [("I", 0)] + [("o" + x, LAST) for x in OUT]
     for t in range(RO):
         tok[("arr", t)] = ("arr%d" % t, arrive)
     head = {k: 0 for k in todo}
@@ -356,10 +430,8 @@ def rank_program(g, core, T, topo):
     def known(dp):
         for x in dp:
             if isinstance(x, tuple) and x[1] < 0:
-                if x[0][0] != "r":
-                    continue
-                x = "c" + x[0][1:]
-            elif isinstance(x, tuple) and x[0] == "left":
+                continue
+            if isinstance(x, tuple) and x[0] == "left":
                 yield ("ls" + "ab"[x[1] % 2], left[x[1]]) if ("S%d" % (NST - 1), x[1]) in tok else "missing"
                 continue
             yield tok.get(x, "missing")
@@ -370,7 +442,7 @@ def rank_program(g, core, T, topo):
         for k in "vspgy":
             while head[k] < len(todo[k]):
                 x, t = todo[k][head[k]]
-                got = list(known(deps(x, t) if k != "y" else [(x[1:], t)]))
+                got = list(known(deps(x, t) if x[0] != "o" else [(x[1:], t)]))
                 if "missing" in got:
                     break
                 need(k, *got)
@@ -378,26 +450,26 @@ def rank_program(g, core, T, topo):
                 if x[0] == "S":
                     send(int(x[1:]), t)
                     tok[nm] = None
-                elif x == "mat":
-                    fin(v.tensor_scalar(T.blkn[:], T.bk2[:, 0:128], -BIG, None, op.mult), "vq")
-                    tok["mat"] = fin(v.tensor_scalar(T.tri[:], T.tri1[:], BIG, None, op.mult), "vq")
-                elif x[0] in "YZ":
-                    buf = E[t % 2] if x == "Y" else U[t % 2]
-                    tok[nm] = fin(g.dma_start(T.RA[:], buf[:], accum_op=op.add), "acc%d" % (2 * t + (x == "Z")), 16)
+                elif x == "I":
+                    tok[nm] = fin(sy.dma_start(T.yp[:], T.RA[:]), "acc0", 16)
+                elif x in "YZ":
+                    buf = U[t % 2] if x == "Z" else T.E0 if t == LAST else E[t % 2]
+                    n = alone(t) if x == "Z" else V
+                    tok[nm] = fin(g.dma_start(T.yp[:, 0:n], buf[:, 0:n], accum_op=op.add), "acc%d" % (2 * t + (x == "Z")), 16)
                 elif x[0] == "o":
                     c = C[int(x[2:])]
-                    if x[1] == "p":
-                        fin(sy.dma_start(T.yp[:, c], T.E1[:, c]), "outp", 16)
-                    else:
-                        fin(sy.dma_start(T.yr[:, c], T.TT[:, c]), "outr", 16)
+                    fin(sy.dma_start(T.yr[:, c], T.W1[:, c]), "outr", 16)
                     tok[nm] = None
                 else:
                     tok[nm] = fin(call(x, t, k), {"v": "vq", "s": "sq", "p": "pq"}[k])
-                    if x[0] == "c" or x in ("nb", "lst"):
+                    if x[0] in "cs" or x == "nb":
                         tok[x] = tok[nm]
+                    if x[0] == "B":
+                        tok[("A" + x[1:], t)] = tok[nm]
                 head[k] += 1
                 more = True
     assert all(head[k] == len(todo[k]) for k in todo), [(k, todo[k][head[k]]) for k in todo if head[k] < len(todo[k])]
-    need("y", ("outp", cnt["outp"]), ("outr", cnt["outr"]))
+    need("y", ("outr", cnt["outr"]))
+    need("g", tok[("Y", LAST)])
     for name in ("vq", "sq", "pq", "gq", "lsa", "lsb"):
         need("g", (name, cnt[name]))

@@ -7,6 +7,7 @@ NS = (N - 1) * G
 NC = NS // 16
 PAD = 8
 BIG = 4096.0
+LOW = 2.0 ** 22
 MAG = 2.0 ** 23
 Q4 = 0.25 * (1.0 - 2.0 ** -23)
 CH = 512
@@ -63,25 +64,25 @@ SCRATCH = {
     "R": ("psum", [128, CH * NB], "float32"),
     "hot": ("psum", [128, CH], "float32"),
 }
+HALF = ("01", "23")
 SEMAPHORES = (["vq", "sq", "pq", "gq", "lsa", "lsb", "lth", "lsn", "lnb", "outr"] + ["lr%d" % c for c in range(NCH)]
-              + ["arr%d" % t for t in range(RO)] + ["acc%d" % k for k in range(2 * RO)])
+              + ["arr%d" % t for t in range(RO)] + ["d%s%d%d" % (a, h, t) for a in "YZ" for h in range(2) for t in range(RO)])
 
 STAGES = ((1,), (2, 2), (2, 2), (2, 2))
 MP = ((0, 256), (256, 512), (768, 512), (1280, 512))
-LOW = 2.0 ** 22
 PARTS = ((0, 6), (6, 4), (10, 4), (14, 2))
 PIECE = {"a": (0, 256), "b": (256, 256), "1": (512, 512), "2": (1024, 512), "3": (1536, 512)}
 
 ORD = {
-    "first": {"v": "c0 sh c1 c2 c3 su B3 sf G0 X0 X1 X2 C0 X3 Q0 L0 M1 M3 b1 b2 nb b0 i0 i1 b3 i2 i3".split(),
-              "s": "A0 A1 A2 G1 G2 G3 W0 H0 e0 W1 M0 M2 W3 W2 e2 e1 e3".split(),
-              "p": "z1 z2 sp z0 P1 P0 P2 P3 K0 n1 n2 z3 n0 n3".split()},
-    "mid": {"v": "tb ua ub u1 u2 r1 u3 r2 r3 X0 G0 X3 X2 H0 C0 X1 Q0 L0 M1 M3 b0 b2 b3 b1 D3 D2".split(),
-            "s": "ta t1 t2 t3 A1 A0 A2 A3 G1 G2 G3 W3 W2 W0 M0 M2 W1 e2 e3 e1 e0".split(),
-            "p": "a0 z1 z0 z2 P1 P0 P2 P3 K0 z3 n0 n3 n1 n2".split()},
-    "last": {"v": "tb ua ub u1 u2 r1 u3 r2 r3 X0 G0 X1 X2 H0 C0 X3 Q0 L0 M1 M3 b0 b1 b2 b3 N0 N2 N3 N1".split(),
-             "s": "ta t1 t2 t3 A1 A0 A2 A3 G1 G2 G3 W0 W2 e0 M0 M2 W3 e2 W1 e3 e1 k1".split(),
-             "p": "a0 z2 z0 z1 P1 P0 P2 P3 K0 z3 n0 n1 y1 n2 n3".split()},
+    "first": {"v": "c0 sh c1 c2 B3 su c3 G0 X1 X23 C0 nb Q0 L0 M1 b2 M3 b1 b0 i0 i12 b3 i3".split(),
+              "s": "h0 A0 A1 A2 sf G1 G2 G3 X0 H0 W01 M0 W2 M2 e01 e2 W3 e3".split(),
+              "p": "z2 j0 z1 sp l0 P1 P0 P2 P3 K0 n2 z0 z3 n3 n0 n1".split()},
+    "mid": {"v": "tb ub ua u1 u2 u3 r2 r3 A3 G0 X0 X2 X3 H0 C0 X1 Q0 L0 M1 b0 b2 b3 W1 b1 D3".split(),
+            "s": "ta t1 t2 t3 A0 A2 A1 G1 G2 G3 W0 W23 M0 M2 M3 e2 e3 e01".split(),
+            "p": "z1 a0 a1 z0 z2 P1 P0 P2 P3 K0 z3 n0 n1 n2 n3".split()},
+    "last": {"v": "tb ta ub ua u1 u2 u3 r2 r3 X0 A1 X3 G0 X1 b0 b1 H0 C0 X2 Q0 L0 M1 M3 b23 N0 N1 N2 N3".split(),
+             "s": "t1 t2 t3 A0 A2 A3 G1 G3 G2 W0 W1 e0 e1 M0 M2 W2 k1 e2 W3 e3".split(),
+             "p": "z1 a0 a1 z0 P1 P0 P2 P3 K0 n0 y1 z3 z2 n1 n3 n2".split()},
     "end": {"v": "u1 u2 ua r2 ub u3 r0 r3".split(),
             "s": "t1 t2 ta tb t3 q1".split(),
             "p": "a1".split()},
@@ -120,25 +121,26 @@ def rank_program(g, core, T, topo):
         return
     v, s, pe, sy = g.vector, g.scalar, g.tensor, g.sync
     eng = {"g": g, "v": v, "s": s, "p": pe, "y": sy}
-    cnt, seen, tok = {}, {}, {}
+    cnt, tok, made, seen = {}, {}, {}, {k: {} for k in eng}
     op, fn = AluOpType, ActivationFunctionType
     NST, LAST = len(STAGES), RO - 1
 
     def need(k, *toks):
-        for name, val in toks:
-            if seen.get((k, name), 0) < val:
+        for name, val in sorted(toks, key=lambda x: -made.get(x, (0, {}))[0]):
+            if seen[k].get(name, 0) < val:
                 eng[k].wait_ge(T.sem[name], val)
-                seen[(k, name)] = val
+                for n2, v2 in list(made.get((name, val), (0, {}))[1].items()) + [(name, val)]:
+                    seen[k][n2] = max(seen[k].get(n2, 0), v2)
 
     def fin(ins, name, n=1):
         cnt[name] = cnt.get(name, 0) + n
         ins.then_inc(T.sem[name], n)
+        if name[1:] == "q":
+            made[(name, cnt[name])] = (len(made) + 1, dict(seen[name[0]]))
         return (name, cnt[name])
 
     o, lane = order(q, T, topo), lanes(q, T, topo)
     arrive = sum(len(lanes((q - d) % N, T, topo)[d]) for d in range(1, N))
-    C = [slice(CH * c, CH * (c + 1)) for c in range(NCH)]
-    CX = [slice(PAD + CH * c, PAD + CH * (c + 1)) for c in range(NCH)]
     W = [T["W%d" % t] for t in range(RO)]
     U, E, OB = [T.U0, T.U1], [T.E0, T.E1], [T.ob0, T.ob1]
     HC, YC = slice(0, NC), slice(128, 128 + NC)
@@ -147,25 +149,39 @@ def rank_program(g, core, T, topo):
     def part(t):
         return ORD[("first", "mid", "mid", "last", "end")[t]]
 
-    def res(c, t):
-        k = (NCH * t + c) % NB
-        return T.R[:, CH * k:CH * (k + 1)]
+    def span(b):
+        return PIECE.get(b) or (CH * int(b[0]), CH * len(b))
+
+    def bank(b):
+        return str(span(b)[0] // CH)
+
+    def half(b):
+        return str(int(bank(b) in HALF[1]))
+
+    def res(b, t):
+        at, n = span(b)
+        k = (NCH * t + at // CH) % NB
+        return T.R[:, CH * k + at % CH:CH * k + at % CH + n]
+
+    def runs(b, t):
+        cut = [k for k in range(1, len(b)) if (NCH * t + int(b[k])) % NB in (0, NB - NCH) or joined(b[k], t) != joined(b[k - 1], t)]
+        return [b[i:j] for i, j in zip([0] + cut, cut + [len(b)])]
 
     def before(c, t):
-        k = NCH * t + c - NB
+        k = NCH * t + int(c) - NB
         return (str(k % NCH), k // NCH)
 
-    def pieces(b):
-        return [x for x in PIECE if PIECE[x][0] // CH == int(b)]
-
     def added(b, t):
-        return "a" + b in part(t + 1)["p"]
+        return [(x, t) for x in part(t + 1)["p"] if x[0] == "a" and bank(x[1:]) == b]
+
+    def summed(b, t):
+        return added(b, t) + [(x, t) for x in part(t + 1)["v"] if x[0] == "r" and bank(x[1:]) == b]
 
     def joined(b, t):
-        return t >= 0 and "D" + b in part(t)["v"]
+        return t >= 0 and any(x[0] == "D" and b[0] in x for x in part(t)["v"])
 
-    def alone(t):
-        return CH * sum(not joined(str(c), t + 1) for c in range(NCH))
+    def alone(h, t):
+        return "".join(c for c in HALF[int(h)] if not joined(c, t + 1))
 
     def send(i, t):
         a, n = sum(map(len, STAGES[:i])), len(STAGES[i])
@@ -191,7 +207,7 @@ def rank_program(g, core, T, topo):
     tok["th"] = fin(s.dma_start(T.thi[:], T.th[:]), "lth", 16)
     tok["sn"] = fin(s.dma_start(T.sni[:], T.snd[:]), "lsn", 16)
     for c in range(NCH):
-        tok["l%d" % c] = fin(sy.dma_start(T.r0i[:, C[c]], T.r0[:, C[c]]), "lr%d" % c, 16)
+        tok["ld%d" % c] = fin(sy.dma_start(T.r0i[:, CH * c:CH * (c + 1)], T.r0[:, CH * c:CH * (c + 1)]), "lr%d" % c, 16)
     tok["nbl"] = fin(sy.dma_start(T.nbi[:], T.nb[:]), "lnb", 16)
     k0 = fin(g.iota(T.col[:], [[0, N - 1], [1, 16]], 0, 0, allow_small_or_imprecise_dtypes=True), "gq")
     need("s", k0)
@@ -211,6 +227,7 @@ def rank_program(g, core, T, topo):
     need("g", k1)
     for k, par in enumerate((T.par0, T.par1)):
         tok["par"] = fin(g.affine_select(par[:], T.up[:], [[0, 4], [1, 2], [0, 16]], op.is_equal, 0.0, -k, 0), "gq")
+    tok["low"] = diag(T.low, T.zb, LOW)
     need("g", kb)
     k2 = fin(g.affine_select(T.bk1[:], T.big[:], [[-16, 9], [0, 16]], op.is_ge, 0.0, 0, 1), "gq")
     need("g", k2)
@@ -230,28 +247,35 @@ def rank_program(g, core, T, topo):
     gp = [str(i) for i in range(len(PARTS))]
     st = [str(i) for i in range(len(MP))]
 
+    def each(a, t, names=al):
+        return [(a + c, t) for c in names]
+
     def deps(x, t):
         a, b = x[0], x[1:]
+        if len(b) > 1:
+            return [y for c in b for y in deps(a + c, t)]
         if a == "c":
-            return ["l" + b]
+            return ["ld" + b]
         if x == "nb":
             return ["nbl"]
         if a == "s":
-            return {"h": ["sn", "zh"], "p": ["par", "sh"], "u": ["sp"], "f": ["sp"]}[b]
+            return {"h": ["sn", "zh"], "p": ["par", "sh"], "u": ["sp"], "f": ["su"]}[b]
+        if a == "B":
+            return ["thf", "ld" + b]
         if a in "Ah":
-            whole = "c" + b if t == 0 else ("a" + b if added(b, t - 1) else "r" + b, t - 1)
+            whole = ["c" + b] if t == 0 else summed(b, t - 1)
             if a == "h":
-                return [whole, ("j" + b, t)] + [("A" + b, t)] * ("A" + b in part(t)["v"])
-            return ["thb", "thc", whole, ("n" + b, t - 1), ("X" + b, t - 1)] + [("G" + i, t - 1) for i in gp]
+                return whole + [("j" + b, t)] + [("A" + b, t) for y in part(t)["v"] if y[0] == "A" and b in y]
+            return ["thb", "thc", ("n" + b, t - 1), ("X" + b, t - 1)] + whole + each("G", t - 1, gp)
         if a == "l":
             return ["low", ("h" + b, t), ("A" + b, t)]
         if a == "X":
-            return ([("A" + b, t), "c" + b, ("W" + b, t - 1), ("b" + b, t - 1)] + [("M" + i, t - 1) for i in st]
+            return ([("A" + b, t), "c" + b, ("W" + b, t - 1), ("b" + b, t - 1)] + each("M", t - 1, st)
                     + [("l" + b, t)] * ("l" + b in part(t)["p"]))
         if a == "W":
             return [("X" + b, t)]
         if a in "zj":
-            pb, pt = before(int(b), t + 1)
+            pb, pt = before(b, t + 1)
             if a == "z" and "l" + b in part(t)["p"]:
                 return [("X" + b, t)]
             return ["zb", ("b" + pb, pt)] + [("i" + pb, pt)] * (pt == 0) + [("D" + pb, pt)] * joined(pb, pt)
@@ -259,35 +283,31 @@ def rank_program(g, core, T, topo):
             return [("z" + b, t), ("X" + b, t)]
         if a == "n":
             return ["down", ("b" + b, t)]
+        if a == "e":
+            return [("W" + b, t), ("b" + b, t) if joined(b, t) else ("Y" + half(b), t - 2) if t > 2 else ("i" + b, t - 2)]
         if a == "i":
             return [("b" + b, t), ("e" + b, t)]
-        if a == "e":
-            return [("W" + b, t), ("b" + b, t) if joined(b, t) else ("Y", t - 2) if t > 2 else ("i" + b, t - 2)]
         if a == "D":
             return [("e" + b, t), ("i" + b, t - 2)]
         if a == "N":
-            return [("e" + b, t), ("n" + b, t), ("Y", t - 1)] + [("k" + b, t)] * added(b, t)
+            return [("e" + b, t), ("n" + b, t), ("Y" + half(b), t - 1)] + [("k" + b, t)] * bool(added(b, t))
         if a == "y":
             return [("b" + b, t)]
         if a == "k":
             return [("y" + b, t), ("n" + b, t)]
         if a == "q":
-            return [("a" + b, t)]
-        if a == "B":
-            return ["thf", "l" + b]
-        if a == "I":
-            return [("i" + c, t) for c in al]
+            return summed(b, t)
         if a == "Y":
-            return ([(("N" if t == LAST else "D" if joined(c, t) else "e") + c, t) for c in al]
-                    + [("Z", t - 1) if alone(t - 1) else ("Y" if t > 1 else "I", t - 1)])
+            return ([(("i" if t == 0 else "N" if t == LAST else "D" if joined(c, t) else "e") + c, t) for c in HALF[int(b)]]
+                    + [(("Z" if alone(b, t - 1) else "Y") + b, t - 1)])
         if a == "Z":
-            return [("u" + c, t) for c in PIECE] + [("Y" if t else "I", t)]
+            return each("u", t, [i for i in PIECE if bank(i) in alone(b, t)]) + [("Y" + b, t)]
         if a == "G":
-            return ["su"] + [("A" + c, t) for c in al] + [("P" + b, t - 1)]
+            return ["su"] + each("A", t) + [("P" + b, t - 1)]
         if a == "P":
             return ["sel", "su", "sf", ("G" + b, t), ("Q0", t - 1)]
         if a == "H":
-            return [("P" + i, t) for i in gp] + [("C0", t - 1), ("K0", t - 1)]
+            return each("P", t, gp) + [("C0", t - 1), ("K0", t - 1)]
         if a == "C":
             return ["rm", ("H0", t), ("K0", t - 1)]
         if a == "K":
@@ -295,24 +315,25 @@ def rank_program(g, core, T, topo):
         if a == "Q":
             return [("K0", t), ("L0", t - 1)]
         if a == "L":
-            return [("Q0", t)] + [("M" + i, t - 1) for i in st]
+            return [("Q0", t)] + each("M", t - 1, st)
         if a == "M":
-            return ["pad", ("L0", t)] + [("X" + c, t) for c in al] + [("left", t - 2)]
+            return ["pad", ("L0", t), ("left", t - 2)] + each("X", t)
         if a == "S":
             lo = G * sum(map(len, STAGES[:int(b)]))
             hi = lo + G * len(STAGES[int(b)])
             return [("M%d" % i, t) for i, (at, n) in enumerate(MP) if at < hi and at + n > lo]
         if a == "t":
-            return ["nb", ("arr", t)] + [("W" + c, t) for c in al] + [("u" + b, t - 1)]
+            return ["nb", ("arr", t), ("u" + b, t - 1)] + each("W", t)
         if a == "u":
-            c = str(PIECE[b][0] // CH)
-            return (["nb", ("arr", t)] + [("W" + c, t) for c in al]
-                    + [("t" + b, t), ("D" + c, t - 1) if joined(c, t - 1) else ("Z", t - 2),
-                       (("a" if added(c, t - 2) else "r") + c, t - 2)])
-        if a == "a":
-            return ["id1", ("k" + b if t == LAST else "n" + b, t)] + [("u" + i, t) for i in pieces(b)]
-        if a == "r":
-            return [("n" + b, t)] + [("u" + i, t) for i in pieces(b)]
+            c = bank(b)
+            return (["nb", ("arr", t), ("t" + b, t), ("D" + c, t - 1) if joined(c, t - 1) else ("Z" + half(c), t - 2)]
+                    + each("W", t) + (summed(c, t - 2) if t > 1 else []))
+        if a in "ar":
+            at, n = span(b)
+            made_by = each("u", t, [i for i in PIECE if at <= PIECE[i][0] < at + n])
+            if a == "a":
+                return ["id1", (("k" if t == LAST else "n") + bank(b), t)] + made_by
+            return [("n" + bank(b), t)] + made_by + added(bank(b), t)
 
     def affine(k, out, src, scale, bias):
         if k == "s":
@@ -321,10 +342,7 @@ def rank_program(g, core, T, topo):
 
     def call(x, t, k):
         a, b = x[0], x[1:]
-        c = int(b) if b.isdigit() else None
         vec = k == "v"
-        if a == "c":
-            return v.tensor_scalar(res(c, 0), T.r0i[:, C[c]], -1.0, None, op.add)
         if x == "nb":
             return v.tensor_copy(T.nbu[:], T.nbi[:])
         if x == "sh":
@@ -343,44 +361,13 @@ def rank_program(g, core, T, topo):
         if x == "su":
             return v.tensor_copy(T.snu[:], T.hot[:, HC])
         if x == "sf":
-            return v.tensor_scalar(T.snf[:], T.hot[:, YC], PAD - (CAP + 1) * BIG, None, op.add)
-        if a == "A":
-            if vec:
-                return v.tensor_scalar(T.F[:, C[c]], res(c, t), T.thc[:], None, op.is_ge)
-            return s.activation(T.F[:, C[c]], res(c, t), fn.Sigmoid, bias=T.thb[:], scale=256.0)
-        if a == "h":
-            return affine(k, res(c, t + 1), res(c, t), 1.0, -LOW)
-        if a == "l":
-            return pe.matmul(res(c, t + 1), T.low[:], T.F[:, C[c]], False, True)
-        if a == "X":
-            if vec:
-                return v.tensor_tensor(T.X[:, CX[c]], res(c, t), T.F[:, C[c]], op.mult)
-            return s.activation(T.X[:, CX[c]], res(c, t + 1), fn.Relu)
-        if a == "W":
-            return affine(k, W[t][:, C[c]], T.X[:, CX[c]], Q4, MAG)
-        if a in "zjy":
-            return pe.matmul(res(c, t + (a != "y")), T.zb[:, 0:128], T.zb[:], True, False)
-        if a == "k":
-            return affine(k, res(c, t), res(c, t + 1), 1.0, 0.0)
-        if a == "q":
-            return affine(k, T.W1[:, C[c]], res(c, t), 1.0, 0.0)
-        if a == "B":
-            return v.tensor_scalar(T.F[:, C[c]], T.r0i[:, C[c]], T.thf[:], None, op.is_ge)
-        if a == "b":
-            return v.tensor_tensor(res(c, t + 1), res(c, t), T.X[:, CX[c]], op.subtract)
-        if a == "n":
-            return pe.matmul(res(c, t + 1), T.down[:], T.F[:, C[c]], False, t == LAST or not added(b, t))
-        if a == "a":
-            return pe.matmul(res(c, t + (t < LAST)), T.id1[:], U[t % 2][:, C[c]], False, True)
-        if a == "r":
-            out = T.W1[:, C[c]] if t == LAST else res(c, t + 1)
-            return v.tensor_tensor(out, U[t % 2][:, C[c]], res(c, t + 1), op.add)
+            return affine(k, T.snf[:], T.hot[:, YC], 1.0, PAD - (CAP + 1) * BIG)
         if a == "G":
-            i, n = PARTS[c]
+            i, n = PARTS[int(b)]
             out, src = T.gs[:, NC * i:NC * (i + n)], T.F[:, 0:V].indirect(T.snu[:, (N - 1) * i:(N - 1) * (i + n)])
             return v.tensor_copy(out, src) if vec else s.activation(out, src, fn.Identity)
         if a == "P":
-            i, n = PARTS[c]
+            i, n = PARTS[int(b)]
             turn = [y for y in part(t)["p"] if y[0] == "P"]
             for j in range(i, i + n):
                 ins = pe.matmul(T.hot[:, HC], T.sel[:, 15 - j:143 - j], T.gs[:, NC * j:NC * (j + 1)],
@@ -398,31 +385,71 @@ def rank_program(g, core, T, topo):
         if a == "L":
             return v.tensor_scalar(T.lstu[:], T.qf[:], (CAP + 1) * BIG, 0.0, op.add, op.max)
         if a == "M":
-            i, n = MP[c]
+            i, n = MP[int(b)]
             return affine(k, OB[t % 2][:, i:i + n], T.X[:, 0:PAD + V].indirect(T.lstu[:, i // 16:(i + n) // 16]), Q4, MAG)
-        if a == "i":
-            return v.tensor_tensor(T.RA[:, C[c]], res(c, 0), T.E0[:, C[c]], op.add)
+        at, n = span(b)
+        cs, cx = slice(at, at + n), slice(PAD + at, PAD + at + n)
+        if a == "c":
+            return v.tensor_scalar(res(b, 0), T.r0i[:, cs], -1.0, None, op.add)
+        if a == "B":
+            return v.tensor_scalar(T.F[:, cs], T.r0i[:, cs], T.thf[:], None, op.is_ge)
+        if a == "A":
+            if vec:
+                return v.tensor_scalar(T.F[:, cs], res(b, t), T.thc[:], None, op.is_ge)
+            return s.activation(T.F[:, cs], res(b, t), fn.Sigmoid, bias=T.thb[:], scale=256.0)
+        if a == "h":
+            return affine(k, res(b, t + 1), res(b, t), 1.0, -LOW)
+        if a == "l":
+            return pe.matmul(res(b, t + 1), T.low[:], T.F[:, cs], False, True)
+        if a == "X":
+            if vec:
+                return v.tensor_tensor(T.X[:, cx], res(b, t), T.F[:, cs], op.mult)
+            return s.activation(T.X[:, cx], res(b, t + 1), fn.Relu)
+        if a == "W":
+            return affine(k, W[t][:, cs], T.X[:, cx], Q4, MAG)
+        if a in "zjy":
+            return pe.matmul(res(b, t + (a != "y")), T.zb[:, 0:128], T.zb[:], True, False)
+        if a == "b":
+            return v.tensor_tensor(res(b, t + 1), res(b, t), T.X[:, cx], op.subtract)
+        if a == "n":
+            return pe.matmul(res(b, t + 1), T.down[:], T.F[:, cs], False, t == LAST or not added(b, t))
+        if a == "t":
+            return affine(k, T.TT[:, cs], W[t][:, 0:V + NS].indirect(T.nbu[:, 128 + at // 16:128 + (at + n) // 16]), 1.0,
+                          (t == LAST) - 2.0 * MAG)
+        if a == "u":
+            return v.tensor_tensor(U[t % 2][:, cs], W[t][:, 0:V + NS].indirect(T.nbu[:, at // 16:(at + n) // 16]), T.TT[:, cs], op.add)
+        if a == "a":
+            return pe.matmul(res(b, t + (t < LAST)), T.id1[:], U[t % 2][:, cs], False, (x, t) == added(bank(b), t)[-1])
+        if a == "r":
+            return v.tensor_tensor(T.W1[:, cs] if t == LAST else res(b, t + 1), U[t % 2][:, cs], res(b, t + 1), op.add)
         if a == "e":
-            return affine(k, res(c, t) if joined(b, t) else E[t % 2][:, C[c]], W[t][:, C[c]], -2.0, 2.0 * MAG)
+            return affine(k, res(b, t) if joined(b, t) else E[t % 2][:, cs], W[t][:, cs], -2.0, 2.0 * MAG)
+        if a == "i":
+            return v.tensor_tensor(T.RA[:, cs], res(b, 0), T.E0[:, cs], op.add)
         if a == "D":
-            return v.tensor_tensor(E[t % 2][:, C[c]], res(c, t), U[(t - 1) % 2][:, C[c]], op.add)
+            return v.tensor_tensor(E[t % 2][:, cs], res(b, t), U[(t - 1) % 2][:, cs], op.add)
         if a == "N":
-            return v.tensor_tensor(T.E0[:, C[c]], T.E1[:, C[c]], res(c, t + 1), op.subtract)
-        if a in "tu":
-            i, n = PIECE[b]
-            cs, i, n = slice(i, i + n), i // 16, n // 16
-            if a == "t":
-                return affine(k, T.TT[:, cs], W[t][:, 0:V + NS].indirect(T.nbu[:, 128 + i:128 + i + n]), 1.0,
-                              (t == LAST) - 2.0 * MAG)
-            return v.tensor_tensor(U[t % 2][:, cs], W[t][:, 0:V + NS].indirect(T.nbu[:, i:i + n]), T.TT[:, cs], op.add)
+            return v.tensor_tensor(T.E0[:, cs], T.E1[:, cs], res(b, t + 1), op.subtract)
+        if a == "k":
+            return affine(k, res(b, t), res(b, t + 1), 1.0, 0.0)
+        if a == "q":
+            return affine(k, T.W1[:, cs], res(b, t), 1.0, 0.0)
+
+    def move(x, t):
+        at, n = span(HALF[int(x[1:])] if x[0] == "Y" else alone(x[1:], t))
+        if x[0] == "Y" and t == 0:
+            return sy.dma_start(T.yp[:, at:at + n], T.RA[:, at:at + n])
+        src = U[t % 2] if x[0] == "Z" else T.E0 if t == LAST else E[t % 2]
+        return g.dma_start(T.yp[:, at:at + n], src[:, at:at + n], accum_op=op.add)
 
     todo = {k: [] for k in "vspgy"}
     for t in range(RO + 1):
         for k in "vsp":
             todo[k] += [(x, t - 1 if x[0] in "tuar" or t == RO else t) for x in part(t)[k]]
     for t in range(RO):
-        todo["g"] += [("Z", t - 1)] * (t > 0 and alone(t - 1) > 0) + [("S%d" % i, t) for i in range(NST)] + [("Y", t)] * (t > 0)
-    todo["y"] += [("I", 0)] + [("o" + x, LAST) for x in OUT]
+        todo["g"] += each("S", t, map(str, range(NST))) + each("Y", t, "01") * (t > 0)
+        todo["g"] += each("Z", t, [h for h in "01" if t < LAST and alone(h, t)])
+    todo["y"] += each("Y", 0, "01") + each("o", LAST, OUT)
     for t in range(RO):
         tok[("arr", t)] = ("arr%d" % t, arrive)
     head = {k: 0 for k in todo}
@@ -446,30 +473,21 @@ def rank_program(g, core, T, topo):
                 if "missing" in got:
                     break
                 need(k, *got)
-                nm = (x, t)
                 if x[0] == "S":
-                    send(int(x[1:]), t)
-                    tok[nm] = None
-                elif x == "I":
-                    tok[nm] = fin(sy.dma_start(T.yp[:], T.RA[:]), "acc0", 16)
-                elif x in "YZ":
-                    buf = U[t % 2] if x == "Z" else T.E0 if t == LAST else E[t % 2]
-                    n = alone(t) if x == "Z" else V
-                    tok[nm] = fin(g.dma_start(T.yp[:, 0:n], buf[:, 0:n], accum_op=op.add), "acc%d" % (2 * t + (x == "Z")), 16)
+                    tok[(x, t)] = send(int(x[1:]), t)
                 elif x[0] == "o":
-                    c = C[int(x[2:])]
-                    fin(sy.dma_start(T.yr[:, c], T.W1[:, c]), "outr", 16)
-                    tok[nm] = None
+                    at, n = span(x[2:])
+                    fin(sy.dma_start(T.yr[:, at:at + n], T.W1[:, at:at + n]), "outr", 16)
+                elif k in "gy":
+                    tok[(x, t)] = fin(move(x, t), "d%s%d" % (x, t), 16)
                 else:
-                    tok[nm] = fin(call(x, t, k), {"v": "vq", "s": "sq", "p": "pq"}[k])
-                    if x[0] in "cs" or x == "nb":
-                        tok[x] = tok[nm]
-                    if x[0] == "B":
-                        tok[("A" + x[1:], t)] = tok[nm]
+                    for b in runs(x[1:], t) if x[0] in "AXbiNrDe" else [x[1:]]:
+                        tok[(x, t)] = tok[x] = fin(call(x[0] + b, t, k), k + "q")
+                    for c in x[1:]:
+                        tok[("A" + c if x[0] == "B" else x[0] + c, t)] = tok[x[0] + c] = tok[x]
                 head[k] += 1
                 more = True
     assert all(head[k] == len(todo[k]) for k in todo), [(k, todo[k][head[k]]) for k in todo if head[k] < len(todo[k])]
     need("y", ("outr", cnt["outr"]))
-    need("g", tok[("Y", LAST)])
-    for name in ("vq", "sq", "pq", "gq", "lsa", "lsb"):
+    for name in ("vq", "sq", "pq", "gq", "lsa", "lsb", "dY0%d" % LAST, "dY1%d" % LAST):
         need("g", (name, cnt[name]))

import numpy as np
from concourse.bass import DstId, RemoteDMATransfer
from concourse.mybir import AluOpType, ActivationFunctionType

V, G, N, RO, CAP = 2048, 256, 8, 4, 64
NS = (N - 1) * G
NC = NS // 16
PAD = 8
BIG = 4096.0
LOW = 2.0 ** 22
MAG = 2.0 ** 23
Q4 = 0.25 * (1.0 - 2.0 ** -23)
CH = 512
NCH = V // CH
NB = 7
SCRATCH = {
    "r0i": ("sbuf", [128, V], "int32"),
    "thi": ("sbuf", [128, 1], "int32"),
    "thb": ("sbuf", [128, 1], "float32"),
    "thf": ("sbuf", [128, 1], "float32"),
    "thc": ("sbuf", [128, 1], "float32"),
    "nbi": ("sbuf", [128, 256], "int32"),
    "nbu": ("sbuf", [128, 256], "uint16"),
    "sni": ("sbuf", [128, NC], "int32"),
    "snh": ("sbuf", [128, NC + 32], "float16"),
    "tr0": ("sbuf", [128, 128], "float16"),
    "tr1": ("sbuf", [128, 128], "float16"),
    "snf": ("sbuf", [128, NC], "float32"),
    "snu": ("sbuf", [128, NC], "uint16"),
    "qf": ("sbuf", [128, NC], "float32"),
    "lstu": ("sbuf", [128, NC], "uint16"),
    "big": ("sbuf", [128, 144], "bfloat16"),
    "zb": ("sbuf", [128, CH], "bfloat16"),
    "zf": ("sbuf", [128, 128], "float32"),
    "bk1": ("sbuf", [128, 144], "bfloat16"),
    "bk2": ("sbuf", [128, 144], "bfloat16"),
    "sel": ("sbuf", [128, 144], "bfloat16"),
    "tri": ("sbuf", [128, 128], "bfloat16"),
    "up": ("sbuf", [128, 128], "bfloat16"),
    "par0": ("sbuf", [128, 128], "bfloat16"),
    "par1": ("sbuf", [128, 128], "bfloat16"),
    "low": ("sbuf", [128, 128], "bfloat16"),
    "down": ("sbuf", [128, 128], "bfloat16"),
    "id1": ("sbuf", [128, 128], "float32"),
    "col": ("sbuf", [128, NC], "float32"),
    "rm": ("sbuf", [128, NC], "bfloat16"),
    "hb": ("sbuf", [128, NC], "bfloat16"),
    "cs": ("sbuf", [128, NC], "bfloat16"),
    "F": ("sbuf", [128, V], "bfloat16"),
    "X": ("sbuf", [128, PAD + V], "float32"),
    "TT": ("sbuf", [128, V], "float32"),
    "RA": ("sbuf", [128, V], "float32"),
    "U0": ("sbuf", [128, V], "float32"),
    "U1": ("sbuf", [128, V], "float32"),
    "E0": ("sbuf", [128, V], "float32"),
    "E1": ("sbuf", [128, V], "float32"),
    "gs": ("sbuf", [128, NS], "bfloat16"),
    "ob0": ("sbuf", [128, NS], "float32"),
    "ob1": ("sbuf", [128, NS], "float32"),
    "W0": ("sbuf", [128, V + NS], "float32"),
    "W1": ("sbuf", [128, V + NS], "float32"),
    "W2": ("sbuf", [128, V + NS], "float32"),
    "W3": ("sbuf", [128, V + NS], "float32"),
    "R": ("psum", [128, CH * NB], "float32"),
    "hot": ("psum", [128, CH], "float32"),
}
HALF = ("01", "23")
SEMAPHORES = (["vq", "sq", "pq", "gq", "lsa", "lsb", "lth", "lsn", "lnb", "outr"] + ["lr%d" % c for c in range(NCH)]
              + ["arr%d" % t for t in range(RO)] + ["d%s%d%d" % (a, h, t) for a in "YZ" for h in range(2) for t in range(RO)])

STAGES = ((1,), (2, 2), (2, 2), (2, 2))
MP = ((0, 256), (256, 512), (768, 512), (1280, 512))
PARTS = ((0, 6), (6, 4), (10, 4), (14, 2))
PIECE = {"a": (0, 256), "b": (256, 256), "1": (512, 512), "2": (1024, 512), "3": (1536, 512)}

ORD = {
    "first": {"v": "c0 sh c1 c2 B3 su c3 G0 X1 X23 C0 nb Q0 L0 M1 b2 M3 b1 b0 i0 i12 b3 i3".split(),
              "s": "h0 A0 A1 A2 sf G1 G2 G3 X0 H0 W01 M0 W2 M2 e01 e2 W3 e3".split(),
              "p": "z2 j0 z1 sp l0 P1 P0 P2 P3 K0 n2 z0 z3 n3 n0 n1".split()},
    "mid": {"v": "tb ub ua u1 u2 u3 r2 r3 A3 G0 X0 X2 X3 H0 C0 X1 Q0 L0 M1 b0 b2 b3 W1 b1 D3".split(),
            "s": "ta t1 t2 t3 A0 A2 A1 G1 G2 G3 W0 W23 M0 M2 M3 e2 e3 e01".split(),
            "p": "z1 a0 a1 z0 z2 P1 P0 P2 P3 K0 z3 n0 n1 n2 n3".split()},
    "last": {"v": "tb ta ub ua u1 u2 u3 r2 r3 X0 A1 X3 G0 X1 b0 b1 H0 C0 X2 Q0 L0 M1 M3 b23 N0 N1 N2 N3".split(),
             "s": "t1 t2 t3 A0 A2 A3 G1 G3 G2 W0 W1 e0 e1 M0 M2 W2 k1 e2 W3 e3".split(),
             "p": "z1 a0 a1 z0 P1 P0 P2 P3 K0 n0 y1 z3 z2 n1 n3 n2".split()},
    "end": {"v": "u1 u2 ua r2 ub u3 r0 r3".split(),
            "s": "t1 t2 ta tb t3 q1".split(),
            "p": "a1".split()},
}
OUT = "r2 q1 r0 r3".split()


def order(q, T, topo):
    far = [d for d in range(1, N) if topo.die(T.cores[(q + d) % N]) != topo.die(T.cores[q])]
    near = [d for d in range(1, N) if d not in far]
    far.sort(key=lambda d: abs(d - N // 2))
    o = []
    for k in range(N):
        if k < len(far):
            o.append(far[k])
        if k < len(near):
            o.append(near[k])
    return o


def lanes(q, T, topo):
    o, res = iter(order(q, T, topo)), {}
    for stage in STAGES:
        used = []
        for n in stage:
            d = next(o)
            e = topo.engines(T.cores[q], T.cores[(q + d) % N])
            res[d] = next(e[k::n] for k in range(n) if e[k] not in used)
            used += res[d]
    return res


def rank_program(g, core, T, topo):
    q = T.rank_of(core)
    if q is None:
        return
    v, s, pe, sy = g.vector, g.scalar, g.tensor, g.sync
    eng = {"g": g, "v": v, "s": s, "p": pe, "y": sy}
    cnt, tok, made, seen = {}, {}, {}, {k: {} for k in eng}
    op, fn = AluOpType, ActivationFunctionType
    NST, LAST = len(STAGES), RO - 1

    def need(k, *toks):
        for name, val in sorted(toks, key=lambda x: -made.get(x, (0, {}))[0]):
            if seen[k].get(name, 0) < val:
                eng[k].wait_ge(T.sem[name], val)
                for n2, v2 in list(made.get((name, val), (0, {}))[1].items()) + [(name, val)]:
                    seen[k][n2] = max(seen[k].get(n2, 0), v2)

    def fin(ins, name, n=1):
        cnt[name] = cnt.get(name, 0) + n
        ins.then_inc(T.sem[name], n)
        if name[1:] == "q":
            made[(name, cnt[name])] = (len(made) + 1, dict(seen[name[0]]))
        return (name, cnt[name])

    o, lane = order(q, T, topo), lanes(q, T, topo)
    arrive = sum(len(lanes((q - d) % N, T, topo)[d]) for d in range(1, N))
    W = [T["W%d" % t] for t in range(RO)]
    U, E, OB = [T.U0, T.U1], [T.E0, T.E1], [T.ob0, T.ob1]
    HC, YC = slice(0, NC), slice(128, 128 + NC)
    left = {}

    def part(t):
        return ORD[("first", "mid", "mid", "last", "end")[t]]

    def span(b):
        return PIECE.get(b) or (CH * int(b[0]), CH * len(b))

    def bank(b):
        return str(span(b)[0] // CH)

    def half(b):
        return str(int(bank(b) in HALF[1]))

    def res(b, t):
        at, n = span(b)
        k = (NCH * t + at // CH) % NB
        return T.R[:, CH * k + at % CH:CH * k + at % CH + n]

    def runs(b, t):
        cut = [k for k in range(1, len(b)) if (NCH * t + int(b[k])) % NB in (0, NB - NCH) or joined(b[k], t) != joined(b[k - 1], t)]
        return [b[i:j] for i, j in zip([0] + cut, cut + [len(b)])]

    def before(c, t):
        k = NCH * t + int(c) - NB
        return (str(k % NCH), k // NCH)

    def added(b, t):
        return [(x, t) for x in part(t + 1)["p"] if x[0] == "a" and bank(x[1:]) == b]

    def summed(b, t):
        return added(b, t) + [(x, t) for x in part(t + 1)["v"] if x[0] == "r" and bank(x[1:]) == b]

    def joined(b, t):
        return t >= 0 and any(x[0] == "D" and b[0] in x for x in part(t)["v"])

    def alone(h, t):
        return "".join(c for c in HALF[int(h)] if not joined(c, t + 1))

    def send(i, t):
        a, n = sum(map(len, STAGES[:i])), len(STAGES[i])
        ls = "ls" + "ab"[t % 2]
        tr = []
        for k in range(n):
            d = o[a + k]
            dst = T.cores[(q + d) % N]
            ad = topo.addr(dst)
            m = sum(1 << e for e in lane[d])
            src = OB[t % 2][:, G * (a + k):G * (a + k + 1)]
            out = W[t][:, V + (d - 1) * G:V + d * G]
            cnt[ls] = cnt.get(ls, 0) + len(lane[d])
            if n == 1:
                g.remote_dma(out, src, T.sem["arr%d" % t], T.sem[ls], ad[1], ad[0], m)
            else:
                tr.append(RemoteDMATransfer(dst_ids=[DstId(rid=ad[0], pnc=ad[1])], dma_engine_mask=m,
                                            remote_sem=T.sem["arr%d" % t], src=src, dst=out))
        if tr:
            g.remote_dma_fused(tr, local_sem=T.sem[ls])
        left[t] = cnt[ls]

    tok["th"] = fin(s.dma_start(T.thi[:], T.th[:]), "lth", 16)
    tok["sn"] = fin(s.dma_start(T.sni[:], T.snd[:]), "lsn", 16)
    for c in range(NCH):
        tok["ld%d" % c] = fin(sy.dma_start(T.r0i[:, CH * c:CH * (c + 1)], T.r0[:, CH * c:CH * (c + 1)]), "lr%d" % c, 16)
    tok["nbl"] = fin(sy.dma_start(T.nbi[:], T.nb[:]), "lnb", 16)
    k0 = fin(g.iota(T.col[:], [[0, N - 1], [1, 16]], 0, 0, allow_small_or_imprecise_dtypes=True), "gq")
    need("s", k0)
    tok["rm"] = fin(s.activation(T.rm[:], T.col[:], fn.Sigmoid, bias=-128.0, scale=256.0), "sq")
    tok["zb"] = fin(v.memset(T.zb[:], 0.0), "vq")
    kb = fin(v.memset(T.big[:], BIG), "vq")
    kf = fin(v.memset(T.zf[:], 0.0), "vq")
    tok["pad"] = fin(v.memset(T.X[:, 0:PAD], 0.0), "vq")
    need("v", tok["zb"])
    tok["zh"] = fin(v.tensor_copy(T.snh[:], T.zb[:, 0:NC + 32]), "vq")

    def diag(out, zero, x):
        return fin(g.affine_select(out[:], zero[:, 0:128], [[-1, 128]], op.not_equal, x, 0, 1), "gq")

    need("g", tok["zb"])
    k1 = diag(T.up, T.zb, 1.0)
    need("g", k1)
    for k, par in enumerate((T.par0, T.par1)):
        tok["par"] = fin(g.affine_select(par[:], T.up[:], [[0, 4], [1, 2], [0, 16]], op.is_equal, 0.0, -k, 0), "gq")
    tok["low"] = diag(T.low, T.zb, LOW)
    need("g", kb)
    k2 = fin(g.affine_select(T.bk1[:], T.big[:], [[-16, 9], [0, 16]], op.is_ge, 0.0, 0, 1), "gq")
    need("g", k2)
    k3 = fin(g.affine_select(T.bk2[:], T.bk1[:], [[16, 9], [0, 16]], op.is_ge, 0.0, 15, -1), "gq")
    need("g", k3)
    tok["sel"] = fin(g.affine_select(T.sel[:], T.bk2[:], [[0, 9], [1, 16]], op.is_equal, 0.0, -15, 0), "gq")
    tok["tri"] = fin(g.affine_select(T.tri[:], T.bk2[:, 0:128], [[-1, 128]], op.is_gt, 0.0, 0, 1), "gq")
    need("g", kf)
    tok["down"] = diag(T.down, T.zb, -1.0)
    tok["id1"] = diag(T.id1, T.zf, 1.0)
    need("v", tok["th"])
    tok["thb"] = fin(v.tensor_scalar(T.thb[:], T.thi[:], -256.0, 384.0, op.mult, op.add), "vq")
    tok["thf"] = fin(v.tensor_copy(T.thf[:], T.thi[:]), "vq")
    tok["thc"] = fin(v.tensor_scalar(T.thc[:], T.thi[:], -1.0, None, op.add), "vq")

    al = [str(c) for c in range(NCH)]
    gp = [str(i) for i in range(len(PARTS))]
    st = [str(i) for i in range(len(MP))]

    def each(a, t, names=al):
        return [(a + c, t) for c in names]

    def deps(x, t):
        a, b = x[0], x[1:]
        if len(b) > 1:
            return [y for c in b for y in deps(a + c, t)]
        if a == "c":
            return ["ld" + b]
        if x == "nb":
            return ["nbl"]
        if a == "s":
            return {"h": ["sn", "zh"], "p": ["par", "sh"], "u": ["sp"], "f": ["su"]}[b]
        if a == "B":
            return ["thf", "ld" + b]
        if a in "Ah":
            whole = ["c" + b] if t == 0 else summed(b, t - 1)
            if a == "h":
                return whole + [("j" + b, t)] + [("A" + b, t) for y in part(t)["v"] if y[0] == "A" and b in y]
            return ["thb", "thc", ("n" + b, t - 1), ("X" + b, t - 1)] + whole + each("G", t - 1, gp)
        if a == "l":
            return ["low", ("h" + b, t), ("A" + b, t)]
        if a == "X":
            return ([("A" + b, t), "c" + b, ("W" + b, t - 1), ("b" + b, t - 1)] + each("M", t - 1, st)
                    + [("l" + b, t)] * ("l" + b in part(t)["p"]))
        if a == "W":
            return [("X" + b, t)]
        if a in "zj":
            pb, pt = before(b, t + 1)
            if a == "z" and "l" + b in part(t)["p"]:
                return [("X" + b, t)]
            return ["zb", ("b" + pb, pt)] + [("i" + pb, pt)] * (pt == 0) + [("D" + pb, pt)] * joined(pb, pt)
        if a == "b":
            return [("z" + b, t), ("X" + b, t)]
        if a == "n":
            return ["down", ("b" + b, t)]
        if a == "e":
            return [("W" + b, t), ("b" + b, t) if joined(b, t) else ("Y" + half(b), t - 2) if t > 2 else ("i" + b, t - 2)]
        if a == "i":
            return [("b" + b, t), ("e" + b, t)]
        if a == "D":
            return [("e" + b, t), ("i" + b, t - 2)]
        if a == "N":
            return [("e" + b, t), ("n" + b, t), ("Y" + half(b), t - 1)] + [("k" + b, t)] * bool(added(b, t))
        if a == "y":
            return [("b" + b, t)]
        if a == "k":
            return [("y" + b, t), ("n" + b, t)]
        if a == "q":
            return summed(b, t)
        if a == "Y":
            return ([(("i" if t == 0 else "N" if t == LAST else "D" if joined(c, t) else "e") + c, t) for c in HALF[int(b)]]
                    + [(("Z" if alone(b, t - 1) else "Y") + b, t - 1)])
        if a == "Z":
            return each("u", t, [i for i in PIECE if bank(i) in alone(b, t)]) + [("Y" + b, t)]
        if a == "G":
            return ["su"] + each("A", t) + [("P" + b, t - 1)]
        if a == "P":
            return ["sel", "su", "sf", ("G" + b, t), ("Q0", t - 1)]
        if a == "H":
            return each("P", t, gp) + [("C0", t - 1), ("K0", t - 1)]
        if a == "C":
            return ["rm", ("H0", t), ("K0", t - 1)]
        if a == "K":
            return ["tri", ("C0", t)]
        if a == "Q":
            return [("K0", t), ("L0", t - 1)]
        if a == "L":
            return [("Q0", t)] + each("M", t - 1, st)
        if a == "M":
            return ["pad", ("L0", t), ("left", t - 2)] + each("X", t)
        if a == "S":
            lo = G * sum(map(len, STAGES[:int(b)]))
            hi = lo + G * len(STAGES[int(b)])
            return [("M%d" % i, t) for i, (at, n) in enumerate(MP) if at < hi and at + n > lo]
        if a == "t":
            return ["nb", ("arr", t), ("u" + b, t - 1)] + each("W", t)
        if a == "u":
            c = bank(b)
            return (["nb", ("arr", t), ("t" + b, t), ("D" + c, t - 1) if joined(c, t - 1) else ("Z" + half(c), t - 2)]
                    + each("W", t) + (summed(c, t - 2) if t > 1 else []))
        if a in "ar":
            at, n = span(b)
            made_by = each("u", t, [i for i in PIECE if at <= PIECE[i][0] < at + n])
            if a == "a":
                return ["id1", (("k" if t == LAST else "n") + bank(b), t)] + made_by
            return [("n" + bank(b), t)] + made_by + added(bank(b), t)

    def affine(k, out, src, scale, bias):
        if k == "s":
            return s.activation(out, src, fn.Identity, bias=bias, scale=scale)
        return v.tensor_scalar(out, src, scale, bias, op.mult, op.add)

    def call(x, t, k):
        a, b = x[0], x[1:]
        vec = k == "v"
        if x == "nb":
            return v.tensor_copy(T.nbu[:], T.nbi[:])
        if x == "sh":
            need("v", fin(v.tensor_copy(T.snh[:, 16:16 + NC], T.sni[:]), "vq"))
            fin(v.transpose(T.tr0[:], T.snh[:, 16:144]), "vq")
            return v.transpose(T.tr1[:], T.snh[:, 0:128])
        if x == "sp":
            for i in range(N - 1):
                d = o[i] - 1
                for par in range(2):
                    at = 16 * d if d % 2 == par else 16 * (d + 1)
                    pe.matmul(T.hot[:, i:NC:N - 1], (T.par0, T.par1)[par][:], (T.tr0 if d % 2 == par else T.tr1)[:, at:at + 16],
                              par == 0, par == 1)
                ins = pe.matmul(T.hot[:, 128 + 16 * i:144 + 16 * i], T.up[:], T.snh[:, 16 + 16 * d:32 + 16 * d], True, True)
            return ins
        if x == "su":
            return v.tensor_copy(T.snu[:], T.hot[:, HC])
        if x == "sf":
            return affine(k, T.snf[:], T.hot[:, YC], 1.0, PAD - (CAP + 1) * BIG)
        if a == "G":
            i, n = PARTS[int(b)]
            out, src = T.gs[:, NC * i:NC * (i + n)], T.F[:, 0:V].indirect(T.snu[:, (N - 1) * i:(N - 1) * (i + n)])
            return v.tensor_copy(out, src) if vec else s.activation(out, src, fn.Identity)
        if a == "P":
            i, n = PARTS[int(b)]
            turn = [y for y in part(t)["p"] if y[0] == "P"]
            for j in range(i, i + n):
                ins = pe.matmul(T.hot[:, HC], T.sel[:, 15 - j:143 - j], T.gs[:, NC * j:NC * (j + 1)],
                                j == i and x == turn[0], j == i + n - 1 and x == turn[-1])
            return ins
        if a == "H":
            return v.tensor_scalar(T.hb[:], T.hot[:, HC], 0.0, None, op.is_gt) if vec else s.activation(T.hb[:], T.hot[:, HC], fn.Sign)
        if a == "C":
            return v.tensor_tensor_scan(T.cs[:], T.rm[:], T.hb[:], 0.0, op.mult, op.subtract)
        if a == "K":
            pe.matmul(T.hot[:, YC], T.tri[:], T.hb[:], True, False)
            return pe.matmul(T.hot[:, YC], T.bk2[:, 0:128], T.cs[:], False, True)
        if a == "Q":
            return v.tensor_tensor(T.qf[:], T.snf[:], T.hot[:, YC], op.min)
        if a == "L":
            return v.tensor_scalar(T.lstu[:], T.qf[:], (CAP + 1) * BIG, 0.0, op.add, op.max)
        if a == "M":
            i, n = MP[int(b)]
            return affine(k, OB[t % 2][:, i:i + n], T.X[:, 0:PAD + V].indirect(T.lstu[:, i // 16:(i + n) // 16]), Q4, MAG)
        at, n = span(b)
        cs, cx = slice(at, at + n), slice(PAD + at, PAD + at + n)
        if a == "c":
            return v.tensor_scalar(res(b, 0), T.r0i[:, cs], -1.0, None, op.add)
        if a == "B":
            return v.tensor_scalar(T.F[:, cs], T.r0i[:, cs], T.thf[:], None, op.is_ge)
        if a == "A":
            if vec:
                return v.tensor_scalar(T.F[:, cs], res(b, t), T.thc[:], None, op.is_ge)
            return s.activation(T.F[:, cs], res(b, t), fn.Sigmoid, bias=T.thb[:], scale=256.0)
        if a == "h":
            return affine(k, res(b, t + 1), res(b, t), 1.0, -LOW)
        if a == "l":
            return pe.matmul(res(b, t + 1), T.low[:], T.F[:, cs], False, True)
        if a == "X":
            if vec:
                return v.tensor_tensor(T.X[:, cx], res(b, t), T.F[:, cs], op.mult)
            return s.activation(T.X[:, cx], res(b, t + 1), fn.Relu)
        if a == "W":
            return affine(k, W[t][:, cs], T.X[:, cx], Q4, MAG)
        if a in "zjy":
            return pe.matmul(res(b, t + (a != "y")), T.zb[:, 0:128], T.zb[:], True, False)
        if a == "b":
            return v.tensor_tensor(res(b, t + 1), res(b, t), T.X[:, cx], op.subtract)
        if a == "n":
            return pe.matmul(res(b, t + 1), T.down[:], T.F[:, cs], False, t == LAST or not added(b, t))
        if a == "t":
            return affine(k, T.TT[:, cs], W[t][:, 0:V + NS].indirect(T.nbu[:, 128 + at // 16:128 + (at + n) // 16]), 1.0,
                          (t == LAST) - 2.0 * MAG)
        if a == "u":
            return v.tensor_tensor(U[t % 2][:, cs], W[t][:, 0:V + NS].indirect(T.nbu[:, at // 16:(at + n) // 16]), T.TT[:, cs], op.add)
        if a == "a":
            return pe.matmul(res(b, t + (t < LAST)), T.id1[:], U[t % 2][:, cs], False, (x, t) == added(bank(b), t)[-1])
        if a == "r":
            return v.tensor_tensor(T.W1[:, cs] if t == LAST else res(b, t + 1), U[t % 2][:, cs], res(b, t + 1), op.add)
        if a == "e":
            return affine(k, res(b, t) if joined(b, t) else E[t % 2][:, cs], W[t][:, cs], -2.0, 2.0 * MAG)
        if a == "i":
            return v.tensor_tensor(T.RA[:, cs], res(b, 0), T.E0[:, cs], op.add)
        if a == "D":
            return v.tensor_tensor(E[t % 2][:, cs], res(b, t), U[(t - 1) % 2][:, cs], op.add)
        if a == "N":
            return v.tensor_tensor(T.E0[:, cs], T.E1[:, cs], res(b, t + 1), op.subtract)
        if a == "k":
            return affine(k, res(b, t), res(b, t + 1), 1.0, 0.0)
        if a == "q":
            return affine(k, T.W1[:, cs], res(b, t), 1.0, 0.0)

    def move(x, t):
        at, n = span(HALF[int(x[1:])] if x[0] == "Y" else alone(x[1:], t))
        if x[0] == "Y" and t == 0:
            return sy.dma_start(T.yp[:, at:at + n], T.RA[:, at:at + n])
        src = U[t % 2] if x[0] == "Z" else T.E0 if t == LAST else E[t % 2]
        return g.dma_start(T.yp[:, at:at + n], src[:, at:at + n], accum_op=op.add)

    todo = {k: [] for k in "vspgy"}
    for t in range(RO + 1):
        for k in "vsp":
            todo[k] += [(x, t - 1 if x[0] in "tuar" or t == RO else t) for x in part(t)[k]]
    for t in range(RO):
        todo["g"] += each("S", t, map(str, range(NST))) + each("Y", t, "01") * (t > 0)
        todo["g"] += each("Z", t, [h for h in "01" if t < LAST and alone(h, t)])
    todo["y"] += each("Y", 0, "01") + each("o", LAST, OUT)
    for t in range(RO):
        tok[("arr", t)] = ("arr%d" % t, arrive)
    head = {k: 0 for k in todo}

    def known(dp):
        for x in dp:
            if isinstance(x, tuple) and x[1] < 0:
                continue
            if isinstance(x, tuple) and x[0] == "left":
                yield ("ls" + "ab"[x[1] % 2], left[x[1]]) if ("S%d" % (NST - 1), x[1]) in tok else "missing"
                continue
            yield tok.get(x, "missing")

    more = True
    while more:
        more = False
        for k in "vspgy":
            while head[k] < len(todo[k]):
                x, t = todo[k][head[k]]
                got = list(known(deps(x, t) if x[0] != "o" else [(x[1:], t)]))
                if "missing" in got:
                    break
                need(k, *got)
                if x[0] == "S":
                    tok[(x, t)] = send(int(x[1:]), t)
                elif x[0] == "o":
                    at, n = span(x[2:])
                    fin(sy.dma_start(T.yr[:, at:at + n], T.W1[:, at:at + n]), "outr", 16)
                elif k in "gy":
                    tok[(x, t)] = fin(move(x, t), "d%s%d" % (x, t), 16)
                else:
                    for b in runs(x[1:], t) if x[0] in "AXbiNrDe" else [x[1:]]:
                        tok[(x, t)] = tok[x] = fin(call(x[0] + b, t, k), k + "q")
                    for c in x[1:]:
                        tok[("A" + c if x[0] == "B" else x[0] + c, t)] = tok[x[0] + c] = tok[x]
                head[k] += 1
                more = True
    assert all(head[k] == len(todo[k]) for k in todo), [(k, todo[k][head[k]]) for k in todo if head[k] < len(todo[k])]
    need("y", ("outr", cnt["outr"]))
    for name in ("vq", "sq", "pq", "gq", "lsa", "lsb", "dY0%d" % LAST, "dY1%d" % LAST):
        need("g", (name, cnt[name]))
